import numpy as np
import ml_dtypes


def mxq(x, axis, fmt="e4m3"):
    dtype, down = {"e4m3": (ml_dtypes.float8_e4m3fn, 7), "e5m2": (ml_dtypes.float8_e5m2, 14)}[fmt]
    v = np.moveaxis(np.asarray(x, np.float32).astype(ml_dtypes.bfloat16).astype(np.float64), axis, -1)
    blocks = v.reshape(v.shape[:-1] + (-1, 32))
    amax = np.abs(blocks).max(-1, keepdims=True)
    byte = np.maximum(np.where(amax > 0, np.frexp(amax)[1] - 1 + 127, 0) - down, 1)
    scale = np.exp2(byte - 127.0)
    codes = (blocks / scale).astype(np.float32).astype(dtype).astype(np.float64)
    return np.moveaxis((codes * scale).reshape(v.shape), -1, axis)


WIDE = False


def mx_kscale(k):
    if not WIDE:
        return np.ones(k)
    levels = np.array([10, -10, 5, -5, 0])
    if k % 512:
        return np.exp2(np.random.permutation(np.resize(levels, k // 32))).repeat(32)
    a = np.empty((k // 512, 16))
    for p in range(k // 512):
        a[p, :8] = np.random.permutation(np.resize(levels, 8))
        for g in range(8):
            far = levels[np.abs(levels - a[p, g]) >= 10]
            a[p, g + 8] = far[np.random.randint(len(far))]
    return np.exp2(a.ravel()).repeat(32)


def f64(x):
    return np.asarray(x).astype(np.float64)


def striped(idx):
    return np.tile(idx.reshape(-1, 16).T, (8, 1)).astype(np.uint16)


def unstriped(offs):
    return offs[:16].T.reshape(-1).astype(np.int64)


E2M1 = np.array([0.0, 0.5, 1.0, 1.5, 2.0, 3.0, 4.0, 6.0, -0.0, -0.5, -1.0, -1.5, -2.0, -3.0, -4.0, -6.0])


def pack_weight(w, fmt):
    k, n = w.shape
    w = f64(np.asarray(w, np.float32).astype(ml_dtypes.bfloat16)).reshape(k // 32, 32, n)
    amax = np.abs(w).max(1)
    if fmt == "e4m3":
        byte = np.frexp(amax)[1] - 1 + 127 - 7
    else:
        mant, ex = np.frexp(amax / 6.0)
        byte = np.where(mant > 0.5, ex, ex - 1) + 127
    byte = np.clip(np.where(amax > 0, byte, 1), 1, 254)
    scaled = (w * np.exp2(127.0 - byte)[:, None, :]).reshape(k, n).astype(np.float32)
    by_word = np.ascontiguousarray(scaled.reshape(k // 512, 128, 4, n).transpose(0, 1, 3, 2))
    if fmt == "e4m3":
        words = by_word.astype(ml_dtypes.float8_e4m3fn).view(np.uint8)
    else:
        c = by_word.astype(ml_dtypes.float4_e2m1fn).view(np.uint8) & 0xF
        words = (c[..., 0::2] | (c[..., 1::2] << 4)).reshape(k // 512, 128, 2 * n)
    return np.ascontiguousarray(words), np.ascontiguousarray(byte.astype(np.uint8).reshape(k // 512, 16, n))


def unpack_weight(words, scales, fmt):
    g, _, n = scales.shape
    words = np.ascontiguousarray(words).reshape(g, 128, n, -1)
    if fmt == "e4m3":
        vals = words.view(ml_dtypes.float8_e4m3fn).astype(np.float64)
    else:
        nib = np.empty((g, 128, n, 4), np.uint8)
        nib[..., 0::2] = words & 0xF
        nib[..., 1::2] = words >> 4
        vals = E2M1[nib]
    vals = vals * np.repeat(np.exp2(scales.astype(np.float64) - 127.0), 8, axis=1)[..., None]
    return vals.transpose(0, 1, 3, 2).reshape(g * 512, n)


def gelu(v):
    return 0.5 * v * (1.0 + np.tanh(np.sqrt(2.0 / np.pi) * (v + 0.044715 * v**3)))


def often(T, S):
    return np.random.permutation(T)[(T * np.random.uniform(0, 1, S) ** 4).astype(np.int64)]


K, K2, H, T, S, P = 512, 1024, 1024, 4096, 1024, 512


def setup_inputs():
    n = np.random.standard_normal
    s = mx_kscale(K)[:, None]
    s2 = mx_kscale(K2)[:, None]
    u = mx_kscale(H)[:, None]
    inp = {}
    inp["tab_words"], inp["tab_scales"] = pack_weight(n((K, T)) * s, "e4m3")
    inp["tab2_words"], inp["tab2_scales"] = pack_weight(n((K2, T)) * s2, "e4m3")
    inp["tab3_words"], inp["tab3_scales"] = pack_weight(n((K, T)) * s, "e4m3")
    inp["offs"] = striped(np.random.permutation(T)[:S])
    inp["offs2"] = striped(np.random.permutation(T)[:S])
    inp["offs3"] = striped(np.random.permutation(T)[:S])
    inp["pos1"] = striped(np.random.permutation(S)[:P])
    inp["pos2"] = striped(often(S, P))
    inp["pos3"] = striped(often(S, P))
    inp["wa"] = (n((K, H)) / K**0.5 / s).astype(np.float32)
    inp["wb_words"], inp["wb_scales"] = pack_weight(n((K2, H)) / K2**0.5 / s2, "e2m1")
    inp["wd_words"], inp["wd_scales"] = pack_weight(n((K, H)) / K**0.5 / s, "e4m3")
    inp["gain"] = (np.exp(0.3 * n(H)) * u[:, 0]).astype(np.float32)
    inp["wo"] = (1.3 * n((H, H)) / H**0.5 / u).astype(np.float32)
    return inp


def reference(tab_words, tab_scales, tab2_words, tab2_scales, tab3_words, tab3_scales, offs, offs2, offs3,
              pos1, pos2, pos3, wa, wb_words, wb_scales, wd_words, wd_scales, gain, wo):
    v = unpack_weight(tab_words, tab_scales, "e4m3")[:, unstriped(offs)]
    v2 = unpack_weight(tab2_words, tab2_scales, "e4m3")[:, unstriped(offs2)]
    v3 = unpack_weight(tab3_words, tab3_scales, "e4m3")[:, unstriped(offs3)]
    a = mxq(f64(wa), 0, "e4m3").T @ v
    b = unpack_weight(wb_words, wb_scales, "e2m1").T @ v2
    d = unpack_weight(wd_words, wd_scales, "e4m3").T @ v3
    bp = b[:, unstriped(pos2)]
    back = np.tanh(a[:, unstriped(pos1)] - bp)
    fore = np.tanh(bp - d[:, unstriped(pos3)])
    z = (back + fore) * f64(gain)[:, None]
    y = mxq(f64(wo), 0, "e4m3").T @ mxq(z, 0, "e4m3")
    return y + bp

@@ -1,0 +1,304 @@
+from contextlib import ExitStack
+
+import concourse.mybir as mybir
+from concourse.masks import make_identity
+
+K, K2, H, T, S, J = 512, 1024, 1024, 4096, 1024, 512
+FLOPS = 2 * (K * H * S + K2 * H * S + K * H * S + H * H * J)
+
+F32 = mybir.dt.float32
+BF16 = mybir.dt.bfloat16
+I32 = mybir.dt.int32
+U32 = mybir.dt.uint32
+U16 = mybir.dt.uint16
+U8 = mybir.dt.uint8
+FP8X4 = mybir.dt.float8_e4m3fn_x4
+FP4X4 = mybir.dt.float4_e2m1fn_x4
+ALU = mybir.AluOpType
+ACT = mybir.ActivationFunctionType
+
+P = 128
+BANK = 512
+TILES = H // P
+GROUP = 4
+JB = J // P
+BANKS = 8
+
+
+KB = 1024
+REG_A, REG_B, REG_C, REG_D, REG_E = 0, 16 * KB, 32 * KB, 48 * KB, 64 * KB
+RING = 80 * KB
+V2_0, V2_1, WA_CODES, V3 = 112 * KB, 116 * KB, 120 * KB, 124 * KB
+WA_BF, WO_BF, Z_BF = 128 * KB, 136 * KB, 152 * KB
+SPARE = 160 * KB
+V2_ROWS = 168 * KB
+X, Y = 0, 4
+
+
+def tile_list_levelling_traverse_features_kernel(
+    tc, tab_words, tab_scales, tab2_words, tab2_scales, tab3_words, tab3_scales, offs, offs2, offs3,
+    pos1, pos2, pos3, wa, wb_words, wb_scales, wd_words, wd_scales, gain, wo, out,
+):
+    nc = tc.nc
+    with ExitStack() as ctx:
+        keep = ctx.enter_context(tc.tile_pool(name="keep", bufs=1))
+        arena = ctx.enter_context(tc.tile_pool(name="arena", bufs=1))
+        psum = ctx.enter_context(tc.psum_pool(name="psum", bufs=1))
+
+        def placed(name, shape, dtype, offset):
+            return arena.tile(shape, dtype, name=name, offset=offset, align_bytes=64)
+
+        def kept(name, shape, dtype):
+            return keep.tile(shape, dtype, name=name, align_bytes=64)
+
+        def bank_tile(name, k):
+            return psum.tile([P, BANK], F32, name=name, tag="bank%d" % k)
+
+        def rows(i):
+            return slice(i * P, (i + 1) * P)
+
+        def load_list(name, src):
+            tile = keep.tile(list(src.shape), U16, name=name)
+            nc.sync.dma_start(tile[:], src)
+            return tile
+
+        def load_words(name, offset, src):
+            tile = placed(name, [P, T], I32, offset)
+            nc.sync.dma_start(out=tile[:], in_=src.rearrange("p t i -> p (t i)").bitcast(I32))
+            return tile
+
+        def load_plane(queue, tile, first, src):
+            for q in range(4):
+                row = 32 * q + first
+                queue.dma_start(out=tile[row : row + 4, :].bitcast(I32), in_=src[4 * q : 4 * q + 4, :].bitcast(I32))
+
+        def gather_words(name, offset, table, offsets, pieces):
+            tile = placed(name, [P, S], U32, offset)
+            n = S // pieces
+            for c in range(pieces):
+                nc.vector.tensor_copy(
+                    tile[:, c * n : (c + 1) * n],
+                    table[:].bitcast(U32).indirect(offsets[:, c * n // 16 : (c + 1) * n // 16]),
+                )
+            return tile
+
+        def load_weight(name, offset, src):
+            raw = placed(name, [P, 2, 4, BANK], F32, offset)
+            for h in range(2):
+                nc.sync.dma_start(
+                    out=raw[:, h], in_=src[:, h * BANK : (h + 1) * BANK].rearrange("(p i) n -> p i n", i=4)
+                )
+            return raw
+
+        def round_weight(name, offset, raw):
+            halves = []
+            for h in range(2):
+                rounded = placed("%s%d" % (name, h), [P, BANK, 4], BF16, offset + 4 * KB * h)
+                nc.gpsimd.tensor_scalar(
+                    out=rounded[:], in0=raw[:, h].rearrange("p i n -> p n i"),
+                    scalar1=1.0, scalar2=0.0, op0=ALU.mult, op1=ALU.add,
+                )
+                halves.append(rounded)
+            return halves
+
+        def quantise_weight(name, offset, halves):
+            codes = placed(name + "_codes", [P, H], U32, offset)
+            scales = kept(name + "_scales", [P, H], U8)
+            for h in range(2):
+                nc.vector.quantize_mx(
+                    out=codes[:, h * BANK : (h + 1) * BANK].bitcast(FP8X4),
+                    scales=scales[:, h * BANK : (h + 1) * BANK],
+                    in_=halves[h][:].rearrange("p n i -> p (n i)"),
+                )
+            return codes, scales
+
+        offs2_sb = load_list("offs2_sb", offs2)
+        offs3_sb = load_list("offs3_sb", offs3)
+        offs_sb = load_list("offs_sb", offs)
+        pos3_sb = load_list("pos3_sb", pos3)
+        pos2_sb = load_list("pos2_sb", pos2)
+        pos1_sb = load_list("pos1_sb", pos1)
+        tab3_sb = load_words("tab3_sb", REG_A, tab3_words[0])
+        wd_sb = kept("wd_sb", [P, H], U32)
+        nc.sync.dma_start(out=wd_sb[:].bitcast(I32), in_=wd_words[0].rearrange("p c i -> p (c i)").bitcast(I32))
+        wb_sb = kept("wb_sb", [P, 2, 2 * H], U8)
+        nc.sync.dma_start(out=wb_sb[:].bitcast(I32), in_=wb_words.rearrange("a p c -> p a c").bitcast(I32))
+
+        tab2_sc = placed("tab2_sc", [P, T], U8, REG_B)
+        tab3_sc = placed("tab3_sc", [P, T], U8, REG_C)
+        tab_sc = placed("tab_sc", [P, T], U8, V2_0)
+        wd_sc = kept("wd_sc", [P, H], U8)
+        wb_sc = kept("wb_sc", [P, 2, H], U8)
+        v2_sc = kept("v2_sc", [P, 2, S], U8)
+        for plane in (tab2_sc, tab3_sc, wd_sc, tab_sc):
+            nc.vector.memset(plane[:].bitcast(I32), 0)
+        for plane in (wb_sc, v2_sc):
+            nc.vector.memset(plane[:].rearrange("p a c -> p (a c)").bitcast(I32), 0)
+        nc.gpsimd.dma_start(
+            out=tab2_sc[0:P:4, :].bitcast(I32), in_=tab2_scales.rearrange("a q t -> (a q) t").bitcast(I32)
+        )
+        load_plane(nc.scalar, tab3_sc, 12, tab3_scales[0])
+        load_plane(nc.scalar, wd_sc, 0, wd_scales[0])
+        load_plane(nc.gpsimd, tab_sc, 8, tab_scales[0])
+        for q in range(4):
+            nc.scalar.dma_start(
+                out=wb_sc[32 * q : 32 * q + 4].bitcast(I32),
+                in_=wb_scales[:, 4 * q : 4 * q + 4, :].rearrange("a r c -> r a c").bitcast(I32),
+            )
+        identity = kept("identity", [P, P], F32)
+        make_identity(nc, identity[:])
+
+        v2_rows = placed("v2_rows", [P, S], U8, V2_ROWS)
+        nc.vector.tensor_copy(v2_rows[:], tab2_sc[:].indirect(offs2_sb[:]))
+        for a in range(2):
+            for r in range(4):
+                nc.gpsimd.dma_start(
+                    out=v2_sc[r:P:32, a, :].bitcast(I32),
+                    in_=v2_rows[64 * a + 4 * r : 64 * (a + 1) : 16, :].bitcast(I32),
+                )
+        v3_sc = kept("v3_sc", [P, S], U8)
+        nc.vector.tensor_copy(v3_sc[:], tab3_sc[:].indirect(offs3_sb[:]))
+        v3 = gather_words("v3", V3, tab3_sb, offs3_sb, 2)
+        v_sc = kept("v_sc", [P, S], U8)
+        nc.vector.tensor_copy(v_sc[:], tab_sc[:].indirect(offs_sb[:]))
+
+        tab2_sb = [load_words("tab2_sb%d" % a, (REG_B, REG_C)[a], tab2_words[a]) for a in range(2)]
+        wa_raw = load_weight("wa_raw", REG_A, wa)
+        gain_sb = placed("gain_sb", [P, 2, 4], F32, V2_ROWS)
+        nc.sync.dma_start(out=gain_sb[:], in_=gain.rearrange("(b p t) -> p b t", p=P, t=4))
+
+        def produce(name, offset, first_bank, passes, sign):
+            window = placed(name, [P, S], F32, offset)
+            for h in range(2):
+                cols = slice(h * BANK, (h + 1) * BANK)
+                bank = bank_tile("%s_bank%d" % (name, h), first_bank + h)
+                for a, (w, w_sc, x, x_sc) in enumerate(passes):
+                    nc.tensor.matmul_mx(
+                        out=bank[:], lhsT=w, lhsT_scale=w_sc, rhs=x[:, cols].bitcast(FP8X4), rhs_scale=x_sc[:, cols],
+                        start=(a == 0), stop=(a == len(passes) - 1),
+                    )
+                nc.scalar.activation(out=window[:, cols], in_=bank[:], func=ACT.Copy, scale=sign)
+            return window
+
+        def pick(name, offset, window, positions):
+            picked = placed(name, [P, J], F32, offset)
+            nc.vector.tensor_copy(picked[:], window[:].indirect(positions[:]))
+            return picked
+
+        def turn(bank, region, src, start, stop):
+            nc.tensor.matmul(bank[:, rows(region)], lhsT=src, rhs=identity[:], is_transpose=True, start=start, stop=stop)
+
+        def differences(name, banks, first, second, sign, offsets):
+            made = []
+            tiles = [bank_tile("%s_bank%d" % (name, jb), banks + jb) for jb in range(JB)]
+            for jb in range(JB):
+                for i in range(GROUP):
+                    turn(tiles[jb], i, first[i][:, rows(jb)], i == 0, False)
+            for i in range(GROUP):
+                for jb in range(JB):
+                    turn(tiles[jb], i, second[i][:, rows(jb)], False, i == GROUP - 1)
+            for jb in range(JB):
+                bounded = placed("%s%d" % (name, jb), [P, 4, P], F32, offsets[jb])
+                nc.scalar.activation(
+                    out=bounded[:], in_=tiles[jb][:].rearrange("j (p t) -> j t p", t=4), func=ACT.Tanh, scale=sign
+                )
+                made.append(bounded)
+            return made
+
+        def ring(k):
+            return RING + 4 * KB * k
+
+        def d_window(i, offset):
+            passes = [(wd_sb[:, rows(i)].bitcast(FP8X4), wd_sc[:, rows(i)], v3, v3_sc[12:P])]
+            return produce("d%d" % i, offset, 2 * i % BANKS, passes, 1.0)
+
+        def b_window(i, offset, first_bank):
+            passes = [
+                (wb_sb[:, a, 2 * i * P : 2 * (i + 1) * P].bitcast(FP4X4), wb_sc[:, a, rows(i)], v2[a], v2_sc[:, a, :])
+                for a in range(2)
+            ]
+            return produce("b%d" % i, offset, first_bank, passes, -1.0)
+
+        def a_window(i, offset):
+            passes = [(wa_codes[:, rows(i)].bitcast(FP8X4), wa_sc[:, rows(i)], v, v_sc[8:P])]
+            return produce("a%d" % i, offset, (Y + 2 * i) % BANKS, passes, 1.0)
+
+        picked_at = [SPARE, REG_B, REG_C, REG_C + 2 * KB] + [REG_D + 2 * KB * i for i in range(GROUP)]
+        neg_b_at = [REG_B + 2 * KB, REG_B + 4 * KB, REG_C + 4 * KB, REG_C + 6 * KB]
+        neg_b_at = neg_b_at + [REG_D + 8 * KB + 2 * KB * i for i in range(GROUP)]
+        fore_at = [[REG_B + 6 * KB + 2 * KB * jb for jb in range(JB)], [REG_C + 8 * KB + 2 * KB * jb for jb in range(JB)]]
+        back_at = [REG_B + 14 * KB] + [SPARE + 2 * KB * jb for jb in range(1, JB)]
+
+        d_win = [d_window(0, REG_D), d_window(1, V2_1), d_window(2, REG_E), d_window(3, REG_E + 4 * KB)]
+        d_win.extend(d_window(i, ring(i)) for i in range(GROUP, TILES))
+        d_picked = [pick("d_picked0", picked_at[0], d_win[0], pos3_sb)]
+        tab_sb = load_words("tab_sb", REG_D, tab_words[0])
+        v2 = [gather_words("v2_0", V2_0, tab2_sb[0], offs2_sb, 1)]
+        d_picked.append(pick("d_picked1", picked_at[1], d_win[1], pos3_sb))
+        v2.append(gather_words("v2_1", V2_1, tab2_sb[1], offs2_sb, 1))
+        d_picked.extend(pick("d_picked%d" % i, picked_at[i], d_win[i], pos3_sb) for i in (2, 3))
+        wo_raw0 = load_weight("wo_raw0", REG_E, wo[0:K, :])
+        wa_bf = round_weight("wa_bf", WA_BF, wa_raw)
+        wo_raw1 = load_weight("wo_raw1", REG_A, wo[K : 2 * K, :])
+        wo_bf = [round_weight("wo_bf0_", WO_BF, wo_raw0), round_weight("wo_bf1_", WO_BF + 8 * KB, wo_raw1)]
+
+        b_win = [b_window(0, ring(0), X), b_window(1, ring(1), X + 2), b_window(2, ring(2), Y), b_window(3, WA_CODES, Y + 2)]
+        neg_b = [pick("neg_b%d" % i, neg_b_at[i], b_win[i], pos2_sb) for i in range(GROUP)]
+        b_win.extend([b_window(4, ring(0), X), b_window(5, ring(1), X + 2)])
+        fore = [differences("fore0_", Y, d_picked, neg_b, -1.0, fore_at[0])]
+        b_win.extend([b_window(6, ring(2), X), b_window(7, ring(3), X + 2)])
+
+        wa_codes, wa_sc = quantise_weight("wa", WA_CODES, wa_bf)
+        v = gather_words("v", WA_BF + 4 * KB, tab_sb, offs_sb, 1)
+        d_picked.extend(pick("d_picked%d" % i, picked_at[i], d_win[i], pos3_sb) for i in range(GROUP, TILES))
+        neg_b.extend(pick("neg_b%d" % i, neg_b_at[i], b_win[i], pos2_sb) for i in range(GROUP, TILES))
+
+        a_win = [a_window(i, ring((GROUP + i) % TILES)) for i in range(TILES)]
+        fore.append(differences("fore1_", Y, d_picked[GROUP:], neg_b[GROUP:], -1.0, fore_at[1]))
+        a_picked = [pick("a_picked%d" % i, picked_at[i], a_win[i], pos1_sb) for i in range(GROUP)]
+        wo_q = [quantise_weight("wo%d" % g, ring(GROUP + 2 * g), wo_bf[g]) for g in range(2)]
+        a_picked.extend(pick("a_picked%d" % i, picked_at[i], a_win[i], pos1_sb) for i in range(GROUP, TILES))
+
+        z_codes = kept("z_codes", [P, 2, J], U32)
+        z_sc = kept("z_sc", [P, 2, J], U8)
+
+        def open_sums(g, banks):
+            tiles = [bank_tile("sum%d_%d" % (g, jb), banks + jb) for jb in range(JB)]
+            for jb in range(JB):
+                for t in range(4):
+                    turn(tiles[jb], t, fore[g][jb][:, t, :], t == 0, False)
+            return tiles
+
+        def finish_z(g, tiles, back):
+            z_bf = placed("z_bf%d" % g, [P, J, 4], BF16, Z_BF + 4 * KB * g)
+            for jb in range(JB):
+                for t in range(4):
+                    turn(tiles[jb], t, back[jb][:, t, :], False, t == 3)
+                nc.vector.tensor_tensor(
+                    out=z_bf[:, rows(jb), :],
+                    in0=tiles[jb][:].rearrange("p (t j) -> p j t", t=4),
+                    in1=gain_sb[:, g, :].unsqueeze(1).to_broadcast([P, P, 4]),
+                    op=ALU.mult,
+                )
+            nc.vector.quantize_mx(
+                out=z_codes[:, g, :].bitcast(FP8X4), scales=z_sc[:, g, :], in_=z_bf[:].rearrange("p j t -> p (j t)")
+            )
+
+        sums = open_sums(0, X)
+        back = differences("back0_", Y, neg_b, a_picked, 1.0, back_at)
+        finish_z(0, sums, back)
+        sums = open_sums(1, Y)
+        back = differences("back1_", X, neg_b[GROUP:], a_picked[GROUP:], 1.0, back_at)
+        finish_z(1, sums, back)
+
+        for i in range(TILES):
+            bank = bank_tile("y%d" % i, X + i)
+            for g in range(2):
+                codes, scales = wo_q[g]
+                nc.tensor.matmul_mx(
+                    out=bank[:], lhsT=codes[:, rows(i)].bitcast(FP8X4), lhsT_scale=scales[:, rows(i)],
+                    rhs=z_codes[:, g, :].bitcast(FP8X4), rhs_scale=z_sc[:, g, :], start=(g == 0), stop=(g == 1),
+                )
+            result = placed("result%d" % i, [P, J], F32, RING + 2 * KB * i)
+            nc.vector.tensor_tensor(out=result[:], in0=bank[:], in1=neg_b[i][:], op=ALU.subtract)
+            nc.sync.dma_start(out=out[rows(i), :], in_=result[:])

@@ -28,10 +28,11 @@ BANKS = 8
 KB = 1024
 REG_A, REG_B, REG_C, REG_D, REG_E = 0, 16 * KB, 32 * KB, 48 * KB, 64 * KB
 RING = 80 * KB
-V2_0, V2_1, WA_CODES, V3 = 112 * KB, 116 * KB, 120 * KB, 124 * KB
+V2_0, V2_1, WA_CODES, V = 112 * KB, 116 * KB, 120 * KB, 124 * KB
 WA_BF, WO_BF, Z_BF = 128 * KB, 136 * KB, 152 * KB
 SPARE = 160 * KB
-V2_ROWS = 168 * KB
+V3 = 168 * KB
+REG_F = 172 * KB
 X, Y = 0, 4
 
 
@@ -90,13 +91,13 @@ def tile_list_levelling_traverse_features_kernel(
                 )
             return raw
 
-        def round_weight(name, offset, raw):
+        def round_weight(name, offset, raw, copy):
             halves = []
             for h in range(2):
                 rounded = placed("%s%d" % (name, h), [P, BANK, 4], BF16, offset + 4 * KB * h)
-                nc.gpsimd.tensor_scalar(
-                    out=rounded[:], in0=raw[:, h].rearrange("p i n -> p n i"),
-                    scalar1=1.0, scalar2=0.0, op0=ALU.mult, op1=ALU.add,
+                copy(
+                    out=rounded[:].rearrange("p (c e) i -> p c i e", e=4),
+                    in_=raw[:, h].rearrange("p i (c e) -> p c i e", e=4),
                 )
                 halves.append(rounded)
             return halves
@@ -112,60 +113,52 @@ def tile_list_levelling_traverse_features_kernel(
                 )
             return codes, scales
 
+        offs_sb = load_list("offs_sb", offs)
         offs2_sb = load_list("offs2_sb", offs2)
         offs3_sb = load_list("offs3_sb", offs3)
-        offs_sb = load_list("offs_sb", offs)
-        pos3_sb = load_list("pos3_sb", pos3)
-        pos2_sb = load_list("pos2_sb", pos2)
         pos1_sb = load_list("pos1_sb", pos1)
-        tab3_sb = load_words("tab3_sb", REG_A, tab3_words[0])
-        wd_sb = kept("wd_sb", [P, H], U32)
-        nc.sync.dma_start(out=wd_sb[:].bitcast(I32), in_=wd_words[0].rearrange("p c i -> p (c i)").bitcast(I32))
-        wb_sb = kept("wb_sb", [P, 2, 2 * H], U8)
-        nc.sync.dma_start(out=wb_sb[:].bitcast(I32), in_=wb_words.rearrange("a p c -> p a c").bitcast(I32))
+        pos2_sb = load_list("pos2_sb", pos2)
+        pos3_sb = load_list("pos3_sb", pos3)
+        wa_raw = load_weight("wa_raw", REG_E, wa)
+        tab_sb = load_words("tab_sb", REG_A, tab_words[0])
 
-        tab2_sc = placed("tab2_sc", [P, T], U8, REG_B)
-        tab3_sc = placed("tab3_sc", [P, T], U8, REG_C)
-        tab_sc = placed("tab_sc", [P, T], U8, V2_0)
+        tab_sc = placed("tab_sc", [P, T], U8, REG_F)
+        tab2_sc = [placed("tab2_sc%d" % a, [P, T], U8, (REG_B, REG_C)[a]) for a in range(2)]
+        tab3_sc = placed("tab3_sc", [P, T], U8, V2_0)
         wd_sc = kept("wd_sc", [P, H], U8)
         wb_sc = kept("wb_sc", [P, 2, H], U8)
-        v2_sc = kept("v2_sc", [P, 2, S], U8)
-        for plane in (tab2_sc, tab3_sc, wd_sc, tab_sc):
+        for plane in (tab_sc, tab2_sc[0], tab2_sc[1], tab3_sc, wd_sc):
             nc.vector.memset(plane[:].bitcast(I32), 0)
-        for plane in (wb_sc, v2_sc):
-            nc.vector.memset(plane[:].rearrange("p a c -> p (a c)").bitcast(I32), 0)
-        nc.gpsimd.dma_start(
-            out=tab2_sc[0:P:4, :].bitcast(I32), in_=tab2_scales.rearrange("a q t -> (a q) t").bitcast(I32)
-        )
-        load_plane(nc.scalar, tab3_sc, 12, tab3_scales[0])
-        load_plane(nc.scalar, wd_sc, 0, wd_scales[0])
-        load_plane(nc.gpsimd, tab_sc, 8, tab_scales[0])
+        nc.vector.memset(wb_sc[:].rearrange("p a c -> p (a c)").bitcast(I32), 0)
+        load_plane(nc.scalar, tab_sc, 8, tab_scales[0])
+        load_plane(nc.gpsimd, tab2_sc[0], 0, tab2_scales[0])
+        load_plane(nc.gpsimd, tab2_sc[1], 0, tab2_scales[1])
+        load_plane(nc.gpsimd, tab3_sc, 12, tab3_scales[0])
         for q in range(4):
-            nc.scalar.dma_start(
+            nc.gpsimd.dma_start(
                 out=wb_sc[32 * q : 32 * q + 4].bitcast(I32),
                 in_=wb_scales[:, 4 * q : 4 * q + 4, :].rearrange("a r c -> r a c").bitcast(I32),
             )
+        load_plane(nc.gpsimd, wd_sc, 0, wd_scales[0])
         identity = kept("identity", [P, P], F32)
         make_identity(nc, identity[:])
 
-        v2_rows = placed("v2_rows", [P, S], U8, V2_ROWS)
-        nc.vector.tensor_copy(v2_rows[:], tab2_sc[:].indirect(offs2_sb[:]))
-        for a in range(2):
-            for r in range(4):
-                nc.gpsimd.dma_start(
-                    out=v2_sc[r:P:32, a, :].bitcast(I32),
-                    in_=v2_rows[64 * a + 4 * r : 64 * (a + 1) : 16, :].bitcast(I32),
-                )
-        v3_sc = kept("v3_sc", [P, S], U8)
-        nc.vector.tensor_copy(v3_sc[:], tab3_sc[:].indirect(offs3_sb[:]))
-        v3 = gather_words("v3", V3, tab3_sb, offs3_sb, 2)
-        v_sc = kept("v_sc", [P, S], U8)
-        nc.vector.tensor_copy(v_sc[:], tab_sc[:].indirect(offs_sb[:]))
+        def gather_scales(name, plane, offsets):
+            tile = kept(name, [P, S], U8)
+            nc.vector.tensor_copy(tile[:], plane[:].indirect(offsets[:]))
+            return tile
 
+        wa_bf = round_weight("wa_bf", WA_BF, wa_raw, nc.scalar.copy)
+        v_sc = gather_scales("v_sc", tab_sc, offs_sb)
+        wo_raw0 = load_weight("wo_raw0", REG_F, wo[0:K, :])
+        v2_sc = [gather_scales("v2_sc0", tab2_sc[0], offs2_sb)]
+        wa_codes, wa_sc = quantise_weight("wa", WA_CODES, wa_bf)
+        v = gather_words("v", V, tab_sb, offs_sb, 2)
+        v2_sc.append(gather_scales("v2_sc1", tab2_sc[1], offs2_sb))
+        v3_sc = gather_scales("v3_sc", tab3_sc, offs3_sb)
         tab2_sb = [load_words("tab2_sb%d" % a, (REG_B, REG_C)[a], tab2_words[a]) for a in range(2)]
-        wa_raw = load_weight("wa_raw", REG_A, wa)
-        gain_sb = placed("gain_sb", [P, 2, 4], F32, V2_ROWS)
-        nc.sync.dma_start(out=gain_sb[:], in_=gain.rearrange("(b p t) -> p b t", p=P, t=4))
+        wb_sb = placed("wb_sb", [P, 2, 2 * H], U8, WA_BF)
+        nc.sync.dma_start(out=wb_sb[:].bitcast(I32), in_=wb_words.rearrange("a p c -> p a c").bitcast(I32))
 
         def produce(name, offset, first_bank, passes, sign):
             window = placed(name, [P, S], F32, offset)
@@ -208,56 +201,58 @@ def tile_list_levelling_traverse_features_kernel(
         def ring(k):
             return RING + 4 * KB * k
 
-        def d_window(i, offset):
-            passes = [(wd_sb[:, rows(i)].bitcast(FP8X4), wd_sc[:, rows(i)], v3, v3_sc[12:P])]
-            return produce("d%d" % i, offset, 2 * i % BANKS, passes, 1.0)
+        def a_window(i, offset):
+            passes = [(wa_codes[:, rows(i)].bitcast(FP8X4), wa_sc[:, rows(i)], v, v_sc[8:P])]
+            return produce("a%d" % i, offset, 2 * i % BANKS, passes, 1.0)
 
         def b_window(i, offset, first_bank):
             passes = [
-                (wb_sb[:, a, 2 * i * P : 2 * (i + 1) * P].bitcast(FP4X4), wb_sc[:, a, rows(i)], v2[a], v2_sc[:, a, :])
+                (wb_sb[:, a, 2 * i * P : 2 * (i + 1) * P].bitcast(FP4X4), wb_sc[:, a, rows(i)], v2[a], v2_sc[a][:])
                 for a in range(2)
             ]
             return produce("b%d" % i, offset, first_bank, passes, -1.0)
 
-        def a_window(i, offset):
-            passes = [(wa_codes[:, rows(i)].bitcast(FP8X4), wa_sc[:, rows(i)], v, v_sc[8:P])]
-            return produce("a%d" % i, offset, (Y + 2 * i) % BANKS, passes, 1.0)
+        def d_window(i, offset):
+            passes = [(wd_sb[:, rows(i)].bitcast(FP8X4), wd_sc[:, rows(i)], v3, v3_sc[12:P])]
+            return produce("d%d" % i, offset, (Y + 2 * i) % BANKS, passes, 1.0)
 
         picked_at = [SPARE, REG_B, REG_C, REG_C + 2 * KB] + [REG_D + 2 * KB * i for i in range(GROUP)]
         neg_b_at = [REG_B + 2 * KB, REG_B + 4 * KB, REG_C + 4 * KB, REG_C + 6 * KB]
         neg_b_at = neg_b_at + [REG_D + 8 * KB + 2 * KB * i for i in range(GROUP)]
-        fore_at = [[REG_B + 6 * KB + 2 * KB * jb for jb in range(JB)], [REG_C + 8 * KB + 2 * KB * jb for jb in range(JB)]]
-        back_at = [REG_B + 14 * KB] + [SPARE + 2 * KB * jb for jb in range(1, JB)]
+        back_at = [[REG_B + 6 * KB + 2 * KB * jb for jb in range(JB)], [REG_C + 8 * KB + 2 * KB * jb for jb in range(JB)]]
+        fore_at = [REG_B + 14 * KB] + [SPARE + 2 * KB * jb for jb in range(1, JB)]
 
-        d_win = [d_window(0, REG_D), d_window(1, V2_1), d_window(2, REG_E), d_window(3, REG_E + 4 * KB)]
-        d_win.extend(d_window(i, ring(i)) for i in range(GROUP, TILES))
-        d_picked = [pick("d_picked0", picked_at[0], d_win[0], pos3_sb)]
-        tab_sb = load_words("tab_sb", REG_D, tab_words[0])
+        a_win = [a_window(0, REG_D), a_window(1, V2_1), a_window(2, REG_E + 8 * KB), a_window(3, ring(3))]
+        wo_bf = [round_weight("wo_bf0_", WO_BF, wo_raw0, nc.scalar.copy)]
+        a_win.extend(a_window(i, ring(i)) for i in range(GROUP, TILES))
+        a_picked = [pick("a_picked0", picked_at[0], a_win[0], pos1_sb)]
+        tab3_sb = load_words("tab3_sb", REG_D, tab3_words[0])
+        gain_sb = placed("gain_sb", [P, 2, 4], F32, REG_E + 4 * KB)
+        nc.sync.dma_start(out=gain_sb[:], in_=gain.rearrange("(b p t) -> p b t", p=P, t=4))
         v2 = [gather_words("v2_0", V2_0, tab2_sb[0], offs2_sb, 1)]
-        d_picked.append(pick("d_picked1", picked_at[1], d_win[1], pos3_sb))
+        a_picked.append(pick("a_picked1", picked_at[1], a_win[1], pos1_sb))
         v2.append(gather_words("v2_1", V2_1, tab2_sb[1], offs2_sb, 1))
-        d_picked.extend(pick("d_picked%d" % i, picked_at[i], d_win[i], pos3_sb) for i in (2, 3))
-        wo_raw0 = load_weight("wo_raw0", REG_E, wo[0:K, :])
-        wa_bf = round_weight("wa_bf", WA_BF, wa_raw)
-        wo_raw1 = load_weight("wo_raw1", REG_A, wo[K : 2 * K, :])
-        wo_bf = [round_weight("wo_bf0_", WO_BF, wo_raw0), round_weight("wo_bf1_", WO_BF + 8 * KB, wo_raw1)]
+        a_picked.extend(pick("a_picked%d" % i, picked_at[i], a_win[i], pos1_sb) for i in (2, 3))
+        wd_sb = placed("wd_sb", [P, H], U32, REG_E + 8 * KB)
+        nc.sync.dma_start(out=wd_sb[:].bitcast(I32), in_=wd_words[0].rearrange("p c i -> p (c i)").bitcast(I32))
+        wo_raw1 = load_weight("wo_raw1", REG_F, wo[K : 2 * K, :])
 
-        b_win = [b_window(0, ring(0), X), b_window(1, ring(1), X + 2), b_window(2, ring(2), Y), b_window(3, WA_CODES, Y + 2)]
+        b_win = [b_window(0, ring(0), X), b_window(1, ring(1), X + 2), b_window(2, ring(2), Y), b_window(3, V3, Y + 2)]
         neg_b = [pick("neg_b%d" % i, neg_b_at[i], b_win[i], pos2_sb) for i in range(GROUP)]
         b_win.extend([b_window(4, ring(0), X), b_window(5, ring(1), X + 2)])
-        fore = [differences("fore0_", Y, d_picked, neg_b, -1.0, fore_at[0])]
+        back = [differences("back0_", Y, a_picked, neg_b, 1.0, back_at[0])]
         b_win.extend([b_window(6, ring(2), X), b_window(7, ring(3), X + 2)])
 
-        wa_codes, wa_sc = quantise_weight("wa", WA_CODES, wa_bf)
-        v = gather_words("v", WA_BF + 4 * KB, tab_sb, offs_sb, 1)
-        d_picked.extend(pick("d_picked%d" % i, picked_at[i], d_win[i], pos3_sb) for i in range(GROUP, TILES))
+        v3 = gather_words("v3", V3, tab3_sb, offs3_sb, 1)
+        a_picked.extend(pick("a_picked%d" % i, picked_at[i], a_win[i], pos1_sb) for i in range(GROUP, TILES))
         neg_b.extend(pick("neg_b%d" % i, neg_b_at[i], b_win[i], pos2_sb) for i in range(GROUP, TILES))
 
-        a_win = [a_window(i, ring((GROUP + i) % TILES)) for i in range(TILES)]
-        fore.append(differences("fore1_", Y, d_picked[GROUP:], neg_b[GROUP:], -1.0, fore_at[1]))
-        a_picked = [pick("a_picked%d" % i, picked_at[i], a_win[i], pos1_sb) for i in range(GROUP)]
-        wo_q = [quantise_weight("wo%d" % g, ring(GROUP + 2 * g), wo_bf[g]) for g in range(2)]
-        a_picked.extend(pick("a_picked%d" % i, picked_at[i], a_win[i], pos1_sb) for i in range(GROUP, TILES))
+        d_win = [d_window(i, ring((GROUP + i) % TILES)) for i in range(TILES)]
+        back.append(differences("back1_", Y, a_picked[GROUP:], neg_b[GROUP:], 1.0, back_at[1]))
+        d_picked = [pick("d_picked%d" % i, picked_at[i], d_win[i], pos3_sb) for i in range(GROUP)]
+        wo_bf.append(round_weight("wo_bf1_", ring(GROUP), wo_raw1, nc.vector.tensor_copy))
+        wo_q = [quantise_weight("wo%d" % g, ring(GROUP + 2 + g), wo_bf[g]) for g in range(2)]
+        d_picked.extend(pick("d_picked%d" % i, picked_at[i], d_win[i], pos3_sb) for i in range(GROUP, TILES))
 
         z_codes = kept("z_codes", [P, 2, J], U32)
         z_sc = kept("z_sc", [P, 2, J], U8)
@@ -266,14 +261,14 @@ def tile_list_levelling_traverse_features_kernel(
             tiles = [bank_tile("sum%d_%d" % (g, jb), banks + jb) for jb in range(JB)]
             for jb in range(JB):
                 for t in range(4):
-                    turn(tiles[jb], t, fore[g][jb][:, t, :], t == 0, False)
+                    turn(tiles[jb], t, back[g][jb][:, t, :], t == 0, False)
             return tiles
 
-        def finish_z(g, tiles, back):
+        def finish_z(g, tiles, fore):
             z_bf = placed("z_bf%d" % g, [P, J, 4], BF16, Z_BF + 4 * KB * g)
             for jb in range(JB):
                 for t in range(4):
-                    turn(tiles[jb], t, back[jb][:, t, :], False, t == 3)
+                    turn(tiles[jb], t, fore[jb][:, t, :], False, t == 3)
                 nc.vector.tensor_tensor(
                     out=z_bf[:, rows(jb), :],
                     in0=tiles[jb][:].rearrange("p (t j) -> p j t", t=4),
@@ -285,11 +280,9 @@ def tile_list_levelling_traverse_features_kernel(
             )
 
         sums = open_sums(0, X)
-        back = differences("back0_", Y, neg_b, a_picked, 1.0, back_at)
-        finish_z(0, sums, back)
+        finish_z(0, sums, differences("fore0_", Y, neg_b, d_picked, -1.0, fore_at))
         sums = open_sums(1, Y)
-        back = differences("back1_", X, neg_b[GROUP:], a_picked[GROUP:], 1.0, back_at)
-        finish_z(1, sums, back)
+        finish_z(1, sums, differences("fore1_", X, neg_b[GROUP:], d_picked[GROUP:], -1.0, fore_at))
 
         for i in range(TILES):
             bank = bank_tile("y%d" % i, X + i)

@@ -33,6 +33,7 @@ WA_BF, WO_BF, Z_BF = 128 * KB, 136 * KB, 152 * KB
 SPARE = 160 * KB
 V3 = 168 * KB
 REG_F = 172 * KB
+WB = 188 * KB
 X, Y = 0, 4
 
 
@@ -83,21 +84,24 @@ def tile_list_levelling_traverse_features_kernel(
                 )
             return tile
 
+        def load_half(raw, src, h):
+            nc.sync.dma_start(
+                out=raw[:, h], in_=src[:, h * BANK : (h + 1) * BANK].rearrange("(p i) n -> p i n", i=4)
+            )
+
         def load_weight(name, offset, src):
             raw = placed(name, [P, 2, 4, BANK], F32, offset)
             for h in range(2):
-                nc.sync.dma_start(
-                    out=raw[:, h], in_=src[:, h * BANK : (h + 1) * BANK].rearrange("(p i) n -> p i n", i=4)
-                )
+                load_half(raw, src, h)
             return raw
 
-        def round_weight(name, offset, raw, copy):
+        def round_weight(name, offset, raw):
             halves = []
             for h in range(2):
                 rounded = placed("%s%d" % (name, h), [P, BANK, 4], BF16, offset + 4 * KB * h)
-                copy(
-                    out=rounded[:].rearrange("p (c e) i -> p c i e", e=4),
-                    in_=raw[:, h].rearrange("p i (c e) -> p c i e", e=4),
+                nc.gpsimd.tensor_scalar(
+                    out=rounded[:], in0=raw[:, h].rearrange("p i n -> p n i"),
+                    scalar1=1.0, scalar2=0.0, op0=ALU.mult, op1=ALU.add,
                 )
                 halves.append(rounded)
             return halves
@@ -113,52 +117,61 @@ def tile_list_levelling_traverse_features_kernel(
                 )
             return codes, scales
 
-        offs_sb = load_list("offs_sb", offs)
-        offs2_sb = load_list("offs2_sb", offs2)
         offs3_sb = load_list("offs3_sb", offs3)
-        pos1_sb = load_list("pos1_sb", pos1)
-        pos2_sb = load_list("pos2_sb", pos2)
+        offs2_sb = load_list("offs2_sb", offs2)
+        offs_sb = load_list("offs_sb", offs)
         pos3_sb = load_list("pos3_sb", pos3)
-        wa_raw = load_weight("wa_raw", REG_E, wa)
-        tab_sb = load_words("tab_sb", REG_A, tab_words[0])
+        pos2_sb = load_list("pos2_sb", pos2)
+        pos1_sb = load_list("pos1_sb", pos1)
+        gain_sb = kept("gain_sb", [P, 2, 4], F32)
+        nc.sync.dma_start(out=gain_sb[:], in_=gain.rearrange("(b p t) -> p b t", p=P, t=4))
+        wd_sb = [kept("wd_sb%d" % h, [P, BANK], U32) for h in range(2)]
+        for h in range(2):
+            nc.sync.dma_start(
+                out=wd_sb[h][:].bitcast(I32),
+                in_=wd_words[0, :, h * BANK : (h + 1) * BANK, :].rearrange("p c i -> p (c i)").bitcast(I32),
+            )
 
-        tab_sc = placed("tab_sc", [P, T], U8, REG_F)
-        tab2_sc = [placed("tab2_sc%d" % a, [P, T], U8, (REG_B, REG_C)[a]) for a in range(2)]
-        tab3_sc = placed("tab3_sc", [P, T], U8, V2_0)
+        tab3_sc = placed("tab3_sc", [P, T], U8, REG_B)
+        tab2_sc = placed("tab2_sc", [P, T], U8, WB)
+        tab_sc = placed("tab_sc", [P, T], U8, REG_C)
         wd_sc = kept("wd_sc", [P, H], U8)
         wb_sc = kept("wb_sc", [P, 2, H], U8)
-        for plane in (tab_sc, tab2_sc[0], tab2_sc[1], tab3_sc, wd_sc):
+        v2_sc1 = kept("v2_sc1", [P, S], U8)
+        for plane in (wd_sc, tab3_sc, tab2_sc, tab_sc, v2_sc1):
             nc.vector.memset(plane[:].bitcast(I32), 0)
         nc.vector.memset(wb_sc[:].rearrange("p a c -> p (a c)").bitcast(I32), 0)
-        load_plane(nc.scalar, tab_sc, 8, tab_scales[0])
-        load_plane(nc.gpsimd, tab2_sc[0], 0, tab2_scales[0])
-        load_plane(nc.gpsimd, tab2_sc[1], 0, tab2_scales[1])
-        load_plane(nc.gpsimd, tab3_sc, 12, tab3_scales[0])
+        load_plane(nc.sync, tab3_sc, 12, tab3_scales[0])
         for q in range(4):
-            nc.gpsimd.dma_start(
+            nc.sync.dma_start(
+                out=tab2_sc[32 * q : 32 * q + 8, :].bitcast(I32), in_=tab2_scales[:, 4 * q : 4 * q + 4, :].bitcast(I32)
+            )
+        load_plane(nc.sync, tab_sc, 8, tab_scales[0])
+        tab3_sb = load_words("tab3_sb", REG_A, tab3_words[0])
+        load_plane(nc.gpsimd, wd_sc, 0, wd_scales[0])
+        for q in range(4):
+            nc.sync.dma_start(
                 out=wb_sc[32 * q : 32 * q + 4].bitcast(I32),
                 in_=wb_scales[:, 4 * q : 4 * q + 4, :].rearrange("a r c -> r a c").bitcast(I32),
             )
-        load_plane(nc.gpsimd, wd_sc, 0, wd_scales[0])
-        identity = kept("identity", [P, P], F32)
-        make_identity(nc, identity[:])
 
         def gather_scales(name, plane, offsets):
             tile = kept(name, [P, S], U8)
             nc.vector.tensor_copy(tile[:], plane[:].indirect(offsets[:]))
             return tile
 
-        wa_bf = round_weight("wa_bf", WA_BF, wa_raw, nc.scalar.copy)
-        v_sc = gather_scales("v_sc", tab_sc, offs_sb)
-        wo_raw0 = load_weight("wo_raw0", REG_F, wo[0:K, :])
-        v2_sc = [gather_scales("v2_sc0", tab2_sc[0], offs2_sb)]
-        wa_codes, wa_sc = quantise_weight("wa", WA_CODES, wa_bf)
-        v = gather_words("v", V, tab_sb, offs_sb, 2)
-        v2_sc.append(gather_scales("v2_sc1", tab2_sc[1], offs2_sb))
         v3_sc = gather_scales("v3_sc", tab3_sc, offs3_sb)
+        v2_sc = [gather_scales("v2_sc0", tab2_sc, offs2_sb), v2_sc1]
+        for r in range(4):
+            nc.gpsimd.dma_start(out=v2_sc1[r:P:32, :].bitcast(I32), in_=v2_sc[0][4 + r : P : 32, :].bitcast(I32))
+        identity = kept("identity", [P, P], F32)
+        make_identity(nc, identity[:])
+        v_sc = gather_scales("v_sc", tab_sc, offs_sb)
         tab2_sb = [load_words("tab2_sb%d" % a, (REG_B, REG_C)[a], tab2_words[a]) for a in range(2)]
-        wb_sb = placed("wb_sb", [P, 2, 2 * H], U8, WA_BF)
+        wb_sb = placed("wb_sb", [P, 2, 2 * H], U8, WB)
         nc.sync.dma_start(out=wb_sb[:].bitcast(I32), in_=wb_words.rearrange("a p c -> p a c").bitcast(I32))
+        v3 = gather_words("v3", V3, tab3_sb, offs3_sb, 2)
+        wa_raw = load_weight("wa_raw", REG_A, wa)
 
         def produce(name, offset, first_bank, passes, sign):
             window = placed(name, [P, S], F32, offset)
@@ -201,9 +214,9 @@ def tile_list_levelling_traverse_features_kernel(
         def ring(k):
             return RING + 4 * KB * k
 
-        def a_window(i, offset):
-            passes = [(wa_codes[:, rows(i)].bitcast(FP8X4), wa_sc[:, rows(i)], v, v_sc[8:P])]
-            return produce("a%d" % i, offset, 2 * i % BANKS, passes, 1.0)
+        def d_window(i, offset):
+            passes = [(wd_sb[i // GROUP][:, rows(i % GROUP)].bitcast(FP8X4), wd_sc[:, rows(i)], v3, v3_sc[12:P])]
+            return produce("d%d" % i, offset, 2 * i % BANKS, passes, 1.0)
 
         def b_window(i, offset, first_bank):
             passes = [
@@ -212,47 +225,49 @@ def tile_list_levelling_traverse_features_kernel(
             ]
             return produce("b%d" % i, offset, first_bank, passes, -1.0)
 
-        def d_window(i, offset):
-            passes = [(wd_sb[:, rows(i)].bitcast(FP8X4), wd_sc[:, rows(i)], v3, v3_sc[12:P])]
-            return produce("d%d" % i, offset, (Y + 2 * i) % BANKS, passes, 1.0)
+        def a_window(i, offset):
+            passes = [(wa_codes[:, rows(i)].bitcast(FP8X4), wa_sc[:, rows(i)], v, v_sc[8:P])]
+            return produce("a%d" % i, offset, (Y + 2 * i) % BANKS, passes, 1.0)
 
-        picked_at = [SPARE, REG_B, REG_C, REG_C + 2 * KB] + [REG_D + 2 * KB * i for i in range(GROUP)]
+        picked_at = [SPARE, SPARE + 2 * KB, REG_B, REG_C, REG_C + 2 * KB, REG_D, REG_D + 2 * KB, REG_D + 4 * KB]
         neg_b_at = [REG_B + 2 * KB, REG_B + 4 * KB, REG_C + 4 * KB, REG_C + 6 * KB]
-        neg_b_at = neg_b_at + [REG_D + 8 * KB + 2 * KB * i for i in range(GROUP)]
-        back_at = [[REG_B + 6 * KB + 2 * KB * jb for jb in range(JB)], [REG_C + 8 * KB + 2 * KB * jb for jb in range(JB)]]
-        fore_at = [REG_B + 14 * KB] + [SPARE + 2 * KB * jb for jb in range(1, JB)]
+        neg_b_at = neg_b_at + [REG_E + 7 * KB, REG_E + 9 * KB, REG_E + 11 * KB, RING + 16 * KB]
+        fore_at = [[base + 8 * KB + 2 * KB * jb for jb in range(JB)] for base in (REG_B, REG_C)]
+        back_at = [SPARE + 4 * KB, SPARE + 6 * KB, REG_B + 6 * KB, REG_D + 14 * KB]
 
-        a_win = [a_window(0, REG_D), a_window(1, V2_1), a_window(2, REG_E + 8 * KB), a_window(3, ring(3))]
-        wo_bf = [round_weight("wo_bf0_", WO_BF, wo_raw0, nc.scalar.copy)]
-        a_win.extend(a_window(i, ring(i)) for i in range(GROUP, TILES))
-        a_picked = [pick("a_picked0", picked_at[0], a_win[0], pos1_sb)]
-        tab3_sb = load_words("tab3_sb", REG_D, tab3_words[0])
-        gain_sb = placed("gain_sb", [P, 2, 4], F32, REG_E + 4 * KB)
-        nc.sync.dma_start(out=gain_sb[:], in_=gain.rearrange("(b p t) -> p b t", p=P, t=4))
+        late_at = [ring(7), ring(7) + 2 * KB, ring(0), ring(0) + 2 * KB]
+
+        def pick_d(first, last):
+            d_picked.extend(pick("d_picked%d" % i, picked_at[i], d_win[i], pos3_sb) for i in range(first, last))
+
+        d_at = [REG_D, V2_0, V2_1, REG_F, ring(0), ring(1), ring(2), ring(3)]
+        d_win = [d_window(i, d_at[i]) for i in range(TILES)]
+        d_picked = []
+        pick_d(0, 2)
+        tab_sb = load_words("tab_sb", REG_D, tab_words[0])
         v2 = [gather_words("v2_0", V2_0, tab2_sb[0], offs2_sb, 1)]
-        a_picked.append(pick("a_picked1", picked_at[1], a_win[1], pos1_sb))
+        pick_d(2, 3)
         v2.append(gather_words("v2_1", V2_1, tab2_sb[1], offs2_sb, 1))
-        a_picked.extend(pick("a_picked%d" % i, picked_at[i], a_win[i], pos1_sb) for i in (2, 3))
-        wd_sb = placed("wd_sb", [P, H], U32, REG_E + 8 * KB)
-        nc.sync.dma_start(out=wd_sb[:].bitcast(I32), in_=wd_words[0].rearrange("p c i -> p (c i)").bitcast(I32))
-        wo_raw1 = load_weight("wo_raw1", REG_F, wo[K : 2 * K, :])
+        pick_d(3, 5)
+        wo_raw0 = load_weight("wo_raw0", REG_F, wo[0:K, :])
+        wa_bf = round_weight("wa_bf", WA_BF, wa_raw)
+        wo_raw1 = load_weight("wo_raw1", REG_A, wo[K : 2 * K, :])
+        wo_bf = [round_weight("wo_bf0_", WO_BF, wo_raw0), round_weight("wo_bf1_", WO_BF + 8 * KB, wo_raw1)]
 
-        b_win = [b_window(0, ring(0), X), b_window(1, ring(1), X + 2), b_window(2, ring(2), Y), b_window(3, V3, Y + 2)]
+        b_win = [b_window(0, ring(4), X), b_window(1, ring(5), X + 2), b_window(2, ring(6), Y), b_window(3, WA_CODES, Y + 2)]
         neg_b = [pick("neg_b%d" % i, neg_b_at[i], b_win[i], pos2_sb) for i in range(GROUP)]
-        b_win.extend([b_window(4, ring(0), X), b_window(5, ring(1), X + 2)])
-        back = [differences("back0_", Y, a_picked, neg_b, 1.0, back_at[0])]
-        b_win.extend([b_window(6, ring(2), X), b_window(7, ring(3), X + 2)])
+        b_win.extend([b_window(4, ring(7), X), b_window(5, ring(0), X + 2)])
+        fore = [differences("fore0_", Y, d_picked, neg_b, -1.0, fore_at[0])]
+        b_win.extend([b_window(6, ring(4), X), b_window(7, ring(5), X + 2)])
 
-        v3 = gather_words("v3", V3, tab3_sb, offs3_sb, 1)
-        a_picked.extend(pick("a_picked%d" % i, picked_at[i], a_win[i], pos1_sb) for i in range(GROUP, TILES))
+        wa_codes, wa_sc = quantise_weight("wa", WA_CODES, wa_bf)
+        v = gather_words("v", WA_BF + 4 * KB, tab_sb, offs_sb, 1)
+        pick_d(5, 8)
+
+        a_at = [ring(6)] + [REG_E + 4 * KB * k for k in range(3)] + [V3] + [ring(k) for k in (1, 2, 3)]
+        a_win = [a_window(i, a_at[i]) for i in range(TILES)]
+        a_picked = [pick("a_picked%d" % i, picked_at[i], a_win[i], pos1_sb) for i in range(GROUP)]
         neg_b.extend(pick("neg_b%d" % i, neg_b_at[i], b_win[i], pos2_sb) for i in range(GROUP, TILES))
-
-        d_win = [d_window(i, ring((GROUP + i) % TILES)) for i in range(TILES)]
-        back.append(differences("back1_", Y, a_picked[GROUP:], neg_b[GROUP:], 1.0, back_at[1]))
-        d_picked = [pick("d_picked%d" % i, picked_at[i], d_win[i], pos3_sb) for i in range(GROUP)]
-        wo_bf.append(round_weight("wo_bf1_", ring(GROUP), wo_raw1, nc.vector.tensor_copy))
-        wo_q = [quantise_weight("wo%d" % g, ring(GROUP + 2 + g), wo_bf[g]) for g in range(2)]
-        d_picked.extend(pick("d_picked%d" % i, picked_at[i], d_win[i], pos3_sb) for i in range(GROUP, TILES))
 
         z_codes = kept("z_codes", [P, 2, J], U32)
         z_sc = kept("z_sc", [P, 2, J], U8)
@@ -261,14 +276,14 @@ def tile_list_levelling_traverse_features_kernel(
             tiles = [bank_tile("sum%d_%d" % (g, jb), banks + jb) for jb in range(JB)]
             for jb in range(JB):
                 for t in range(4):
-                    turn(tiles[jb], t, back[g][jb][:, t, :], t == 0, False)
+                    turn(tiles[jb], t, fore[g][jb][:, t, :], t == 0, False)
             return tiles
 
-        def finish_z(g, tiles, fore):
+        def finish_z(g, tiles, back):
             z_bf = placed("z_bf%d" % g, [P, J, 4], BF16, Z_BF + 4 * KB * g)
             for jb in range(JB):
                 for t in range(4):
-                    turn(tiles[jb], t, fore[jb][:, t, :], False, t == 3)
+                    turn(tiles[jb], t, back[jb][:, t, :], False, t == 3)
                 nc.vector.tensor_tensor(
                     out=z_bf[:, rows(jb), :],
                     in0=tiles[jb][:].rearrange("p (t j) -> p j t", t=4),
@@ -279,10 +294,27 @@ def tile_list_levelling_traverse_features_kernel(
                 out=z_codes[:, g, :].bitcast(FP8X4), scales=z_sc[:, g, :], in_=z_bf[:].rearrange("p j t -> p (j t)")
             )
 
-        sums = open_sums(0, X)
-        finish_z(0, sums, differences("fore0_", Y, neg_b, d_picked, -1.0, fore_at))
-        sums = open_sums(1, Y)
-        finish_z(1, sums, differences("fore1_", X, neg_b[GROUP:], d_picked[GROUP:], -1.0, fore_at))
+        back = differences("back0_", Y, neg_b, a_picked, 1.0, back_at)
+        planes = placed("z_planes", [P, 4, J], BF16, WA_BF)
+        for t in range(4):
+            bank = bank_tile("sum0_%d" % t, X + t)
+            for jb in range(JB):
+                turn(bank, jb, fore[0][jb][:, t, :], jb == 0, False)
+            for jb in range(JB):
+                turn(bank, jb, back[jb][:, t, :], False, jb == JB - 1)
+            nc.scalar.activation(out=planes[:, t, :], in_=bank[:], func=ACT.Copy, scale=gain_sb[:, 0, t : t + 1])
+        z_bf0 = placed("z_bf0", [P, J, 4], BF16, Z_BF)
+        nc.gpsimd.tensor_scalar(
+            out=z_bf0[:], in0=planes[:].rearrange("p t j -> p j t"), scalar1=1.0, scalar2=0.0, op0=ALU.mult, op1=ALU.add
+        )
+        fore.append(differences("fore1_", Y, d_picked[GROUP:], neg_b[GROUP:], -1.0, fore_at[1]))
+        a_picked.extend(pick("a_picked%d" % i, late_at[i - GROUP], a_win[i], pos1_sb) for i in range(GROUP, TILES))
+        wo_q = [quantise_weight("wo%d" % g, a_at[TILES - 2 + g], wo_bf[g]) for g in range(2)]
+        nc.vector.quantize_mx(
+            out=z_codes[:, 0, :].bitcast(FP8X4), scales=z_sc[:, 0, :], in_=z_bf0[:].rearrange("p j t -> p (j t)")
+        )
+        back = differences("back1_", X, neg_b[GROUP:], a_picked[GROUP:], 1.0, back_at)
+        finish_z(1, open_sums(1, Y), back)
 
         for i in range(TILES):
             bank = bank_tile("y%d" % i, X + i)
@@ -292,6 +324,6 @@ def tile_list_levelling_traverse_features_kernel(
                     out=bank[:], lhsT=codes[:, rows(i)].bitcast(FP8X4), lhsT_scale=scales[:, rows(i)],
                     rhs=z_codes[:, g, :].bitcast(FP8X4), rhs_scale=z_sc[:, g, :], start=(g == 0), stop=(g == 1),
                 )
-            result = placed("result%d" % i, [P, J], F32, RING + 2 * KB * i)
+            result = placed("result%d" % i, [P, J], F32, REG_F + 2 * KB * i)
             nc.vector.tensor_tensor(out=result[:], in0=bank[:], in1=neg_b[i][:], op=ALU.subtract)
             nc.sync.dma_start(out=out[rows(i), :], in_=result[:])

@@ -34,7 +34,10 @@ SPARE = 160 * KB
 V3 = 168 * KB
 REG_F = 172 * KB
 WB = 188 * KB
+REG_G = 192 * KB
 X, Y = 0, 4
+AS_IS = "j (t p) -> j t p"
+BY_BYTE = "j (p t) -> j t p"
 
 
 def tile_list_levelling_traverse_features_kernel(
@@ -123,8 +126,8 @@ def tile_list_levelling_traverse_features_kernel(
         pos3_sb = load_list("pos3_sb", pos3)
         pos2_sb = load_list("pos2_sb", pos2)
         pos1_sb = load_list("pos1_sb", pos1)
-        gain_sb = kept("gain_sb", [P, 2, 4], F32)
-        nc.sync.dma_start(out=gain_sb[:], in_=gain.rearrange("(b p t) -> p b t", p=P, t=4))
+        gain_sb = kept("gain_sb", [P, 4], F32)
+        nc.sync.dma_start(out=gain_sb[:], in_=gain[K : 2 * K].rearrange("(p t) -> p t", t=4))
         wd_sb = [kept("wd_sb%d" % h, [P, BANK], U32) for h in range(2)]
         for h in range(2):
             nc.sync.dma_start(
@@ -194,7 +197,7 @@ def tile_list_levelling_traverse_features_kernel(
         def turn(bank, region, src, start, stop):
             nc.tensor.matmul(bank[:, rows(region)], lhsT=src, rhs=identity[:], is_transpose=True, start=start, stop=stop)
 
-        def differences(name, banks, first, second, sign, offsets):
+        def differences(name, banks, first, second, sign, offsets, order):
             made = []
             tiles = [bank_tile("%s_bank%d" % (name, jb), banks + jb) for jb in range(JB)]
             for jb in range(JB):
@@ -206,7 +209,7 @@ def tile_list_levelling_traverse_features_kernel(
             for jb in range(JB):
                 bounded = placed("%s%d" % (name, jb), [P, 4, P], F32, offsets[jb])
                 nc.scalar.activation(
-                    out=bounded[:], in_=tiles[jb][:].rearrange("j (p t) -> j t p", t=4), func=ACT.Tanh, scale=sign
+                    out=bounded[:], in_=tiles[jb][:].rearrange(order, t=4), func=ACT.Tanh, scale=sign
                 )
                 made.append(bounded)
             return made
@@ -231,16 +234,16 @@ def tile_list_levelling_traverse_features_kernel(
 
         picked_at = [SPARE, SPARE + 2 * KB, REG_B, REG_C, REG_C + 2 * KB, REG_D, REG_D + 2 * KB, REG_D + 4 * KB]
         neg_b_at = [REG_B + 2 * KB, REG_B + 4 * KB, REG_C + 4 * KB, REG_C + 6 * KB]
-        neg_b_at = neg_b_at + [REG_E + 7 * KB, REG_E + 9 * KB, REG_E + 11 * KB, RING + 16 * KB]
+        neg_b_at = neg_b_at + [REG_D + 6 * KB + 2 * KB * i for i in range(GROUP)]
         fore_at = [[base + 8 * KB + 2 * KB * jb for jb in range(JB)] for base in (REG_B, REG_C)]
         back_at = [SPARE + 4 * KB, SPARE + 6 * KB, REG_B + 6 * KB, REG_D + 14 * KB]
 
-        late_at = [ring(7), ring(7) + 2 * KB, ring(0), ring(0) + 2 * KB]
+        late_back_at = [REG_A + 8 * KB + 2 * KB * jb for jb in range(JB)]
 
         def pick_d(first, last):
             d_picked.extend(pick("d_picked%d" % i, picked_at[i], d_win[i], pos3_sb) for i in range(first, last))
 
-        d_at = [REG_D, V2_0, V2_1, REG_F, ring(0), ring(1), ring(2), ring(3)]
+        d_at = [REG_D, V2_0, V2_1, REG_F, REG_G, ring(1), ring(2), ring(3)]
         d_win = [d_window(i, d_at[i]) for i in range(TILES)]
         d_picked = []
         pick_d(0, 2)
@@ -250,71 +253,72 @@ def tile_list_levelling_traverse_features_kernel(
         v2.append(gather_words("v2_1", V2_1, tab2_sb[1], offs2_sb, 1))
         pick_d(3, 5)
         wo_raw0 = load_weight("wo_raw0", REG_F, wo[0:K, :])
+        gain_row = placed("gain_row", [P, K], F32, REG_G)
+        nc.sync.dma_start(out=gain_row[:], in_=gain[0:K].partition_broadcast(P))
         wa_bf = round_weight("wa_bf", WA_BF, wa_raw)
         wo_raw1 = load_weight("wo_raw1", REG_A, wo[K : 2 * K, :])
-        wo_bf = [round_weight("wo_bf0_", WO_BF, wo_raw0), round_weight("wo_bf1_", WO_BF + 8 * KB, wo_raw1)]
 
         b_win = [b_window(0, ring(4), X), b_window(1, ring(5), X + 2), b_window(2, ring(6), Y), b_window(3, WA_CODES, Y + 2)]
         neg_b = [pick("neg_b%d" % i, neg_b_at[i], b_win[i], pos2_sb) for i in range(GROUP)]
         b_win.extend([b_window(4, ring(7), X), b_window(5, ring(0), X + 2)])
-        fore = [differences("fore0_", Y, d_picked, neg_b, -1.0, fore_at[0])]
+        fore = [differences("fore0_", Y, d_picked, neg_b, -1.0, fore_at[0], AS_IS)]
         b_win.extend([b_window(6, ring(4), X), b_window(7, ring(5), X + 2)])
 
         wa_codes, wa_sc = quantise_weight("wa", WA_CODES, wa_bf)
-        v = gather_words("v", WA_BF + 4 * KB, tab_sb, offs_sb, 1)
+        v = gather_words("v", WA_BF, tab_sb, offs_sb, 1)
+        wo_bf = [round_weight("wo_bf0_", WA_BF + 4 * KB, wo_raw0), round_weight("wo_bf1_", WA_BF + 12 * KB, wo_raw1)]
         pick_d(5, 8)
-
-        a_at = [ring(6)] + [REG_E + 4 * KB * k for k in range(3)] + [V3] + [ring(k) for k in (1, 2, 3)]
-        a_win = [a_window(i, a_at[i]) for i in range(TILES)]
-        a_picked = [pick("a_picked%d" % i, picked_at[i], a_win[i], pos1_sb) for i in range(GROUP)]
         neg_b.extend(pick("neg_b%d" % i, neg_b_at[i], b_win[i], pos2_sb) for i in range(GROUP, TILES))
+
+        a_at = [ring(k) for k in (6, 1, 2, 3, 7, 0, 4, 5)]
+        a_win = [a_window(i, a_at[i]) for i in range(TILES)]
+        fore.append(differences("fore1_", Y, d_picked[GROUP:], neg_b[GROUP:], -1.0, fore_at[1], BY_BYTE))
+        a_picked = [pick("a_picked%d" % i, picked_at[i], a_win[i], pos1_sb) for i in range(TILES)]
+        wo_q = [quantise_weight("wo%d" % g, a_at[(3, 7)[g]], wo_bf[g]) for g in range(2)]
 
         z_codes = kept("z_codes", [P, 2, J], U32)
         z_sc = kept("z_sc", [P, 2, J], U8)
 
-        def open_sums(g, banks):
-            tiles = [bank_tile("sum%d_%d" % (g, jb), banks + jb) for jb in range(JB)]
-            for jb in range(JB):
-                for t in range(4):
-                    turn(tiles[jb], t, fore[g][jb][:, t, :], t == 0, False)
-            return tiles
-
-        def finish_z(g, tiles, back):
-            z_bf = placed("z_bf%d" % g, [P, J, 4], BF16, Z_BF + 4 * KB * g)
-            for jb in range(JB):
-                for t in range(4):
-                    turn(tiles[jb], t, back[jb][:, t, :], False, t == 3)
-                nc.vector.tensor_tensor(
-                    out=z_bf[:, rows(jb), :],
-                    in0=tiles[jb][:].rearrange("p (t j) -> p j t", t=4),
-                    in1=gain_sb[:, g, :].unsqueeze(1).to_broadcast([P, P, 4]),
-                    op=ALU.mult,
-                )
+        def quantise_z(g, z_bf):
             nc.vector.quantize_mx(
                 out=z_codes[:, g, :].bitcast(FP8X4), scales=z_sc[:, g, :], in_=z_bf[:].rearrange("p j t -> p (j t)")
             )
 
-        back = differences("back0_", Y, neg_b, a_picked, 1.0, back_at)
-        planes = placed("z_planes", [P, 4, J], BF16, WA_BF)
-        for t in range(4):
-            bank = bank_tile("sum0_%d" % t, X + t)
-            for jb in range(JB):
-                turn(bank, jb, fore[0][jb][:, t, :], jb == 0, False)
-            for jb in range(JB):
-                turn(bank, jb, back[jb][:, t, :], False, jb == JB - 1)
-            nc.scalar.activation(out=planes[:, t, :], in_=bank[:], func=ACT.Copy, scale=gain_sb[:, 0, t : t + 1])
-        z_bf0 = placed("z_bf0", [P, J, 4], BF16, Z_BF)
-        nc.gpsimd.tensor_scalar(
-            out=z_bf0[:], in0=planes[:].rearrange("p t j -> p j t"), scalar1=1.0, scalar2=0.0, op0=ALU.mult, op1=ALU.add
-        )
-        fore.append(differences("fore1_", Y, d_picked[GROUP:], neg_b[GROUP:], -1.0, fore_at[1]))
-        a_picked.extend(pick("a_picked%d" % i, late_at[i - GROUP], a_win[i], pos1_sb) for i in range(GROUP, TILES))
-        wo_q = [quantise_weight("wo%d" % g, a_at[TILES - 2 + g], wo_bf[g]) for g in range(2)]
-        nc.vector.quantize_mx(
-            out=z_codes[:, 0, :].bitcast(FP8X4), scales=z_sc[:, 0, :], in_=z_bf0[:].rearrange("p j t -> p (j t)")
-        )
-        back = differences("back1_", X, neg_b[GROUP:], a_picked[GROUP:], 1.0, back_at)
-        finish_z(1, open_sums(1, Y), back)
+        z_bf = [placed("z_bf%d" % g, [P, J, 4], BF16, Z_BF + 4 * KB * g) for g in range(2)]
+        back0 = differences("back0_", X, neg_b, a_picked, 1.0, back_at, AS_IS)
+        totals = []
+        for jb in range(JB):
+            total = placed("total%d" % jb, [P, BANK], F32, REG_A + 2 * KB * jb)
+            nc.gpsimd.tensor_tensor(
+                out=total[:], in0=fore[0][jb][:].rearrange("j t p -> j (t p)"),
+                in1=back0[jb][:].rearrange("j t p -> j (t p)"), op=ALU.add,
+            )
+            totals.append(total)
+        sums = [bank_tile("sum%d" % jb, Y + jb) for jb in range(JB)]
+        for jb in range(JB):
+            for t in range(4):
+                turn(sums[jb], t, fore[1][jb][:, t, :], t == 0, False)
+        back1 = differences("back1_", X, neg_b[GROUP:], a_picked[GROUP:], 1.0, late_back_at, BY_BYTE)
+        for jb in range(JB):
+            z_t = placed("z_t%d" % jb, [P, BANK], BF16, REG_G + 2 * KB + KB * jb)
+            nc.vector.tensor_tensor(out=z_t[:], in0=totals[jb][:], in1=gain_row[:], op=ALU.mult)
+            bank = bank_tile("z_bank%d" % jb, X + jb)
+            for u in range(2):
+                nc.tensor.transpose(bank[:, rows(u)], z_t[:].bitcast(F32)[:, u : 2 * P : 2], identity[:])
+            nc.scalar.copy(
+                out=z_bf[0][:, rows(jb), :].bitcast(F32), in_=bank[:, 0 : 2 * P].rearrange("p (u j) -> p j u", u=2)
+            )
+        for jb in range(JB):
+            for t in range(4):
+                turn(sums[jb], t, back1[jb][:, t, :], False, t == 3)
+            nc.vector.tensor_tensor(
+                out=z_bf[1][:, rows(jb), :],
+                in0=sums[jb][:].rearrange("p (t j) -> p j t", t=4),
+                in1=gain_sb[:].unsqueeze(1).to_broadcast([P, P, 4]),
+                op=ALU.mult,
+            )
+        quantise_z(0, z_bf[0])
+        quantise_z(1, z_bf[1])
 
         for i in range(TILES):
             bank = bank_tile("y%d" % i, X + i)
@@ -324,6 +328,6 @@ def tile_list_levelling_traverse_features_kernel(
                     out=bank[:], lhsT=codes[:, rows(i)].bitcast(FP8X4), lhsT_scale=scales[:, rows(i)],
                     rhs=z_codes[:, g, :].bitcast(FP8X4), rhs_scale=z_sc[:, g, :], start=(g == 0), stop=(g == 1),
                 )
-            result = placed("result%d" % i, [P, J], F32, REG_F + 2 * KB * i)
+            result = placed("result%d" % i, [P, J], F32, REG_E + 2 * KB * i)
             nc.vector.tensor_tensor(out=result[:], in0=bank[:], in1=neg_b[i][:], op=ALU.subtract)
             nc.sync.dma_start(out=out[rows(i), :], in_=result[:])

@@ -34,10 +34,7 @@ SPARE = 160 * KB
 V3 = 168 * KB
 REG_F = 172 * KB
 WB = 188 * KB
-REG_G = 192 * KB
 X, Y = 0, 4
-AS_IS = "j (t p) -> j t p"
-BY_BYTE = "j (p t) -> j t p"
 
 
 def tile_list_levelling_traverse_features_kernel(
@@ -126,8 +123,8 @@ def tile_list_levelling_traverse_features_kernel(
         pos3_sb = load_list("pos3_sb", pos3)
         pos2_sb = load_list("pos2_sb", pos2)
         pos1_sb = load_list("pos1_sb", pos1)
-        gain_sb = kept("gain_sb", [P, 4], F32)
-        nc.sync.dma_start(out=gain_sb[:], in_=gain[K : 2 * K].rearrange("(p t) -> p t", t=4))
+        gain_sb = kept("gain_sb", [P, 2, 4], F32)
+        nc.sync.dma_start(out=gain_sb[:], in_=gain.rearrange("(b p t) -> p b t", p=P, t=4))
         wd_sb = [kept("wd_sb%d" % h, [P, BANK], U32) for h in range(2)]
         for h in range(2):
             nc.sync.dma_start(
@@ -197,7 +194,7 @@ def tile_list_levelling_traverse_features_kernel(
         def turn(bank, region, src, start, stop):
             nc.tensor.matmul(bank[:, rows(region)], lhsT=src, rhs=identity[:], is_transpose=True, start=start, stop=stop)
 
-        def differences(name, banks, first, second, sign, offsets, order):
+        def differences(name, banks, first, second, sign, offsets):
             made = []
             tiles = [bank_tile("%s_bank%d" % (name, jb), banks + jb) for jb in range(JB)]
             for jb in range(JB):
@@ -209,7 +206,7 @@ def tile_list_levelling_traverse_features_kernel(
             for jb in range(JB):
                 bounded = placed("%s%d" % (name, jb), [P, 4, P], F32, offsets[jb])
                 nc.scalar.activation(
-                    out=bounded[:], in_=tiles[jb][:].rearrange(order, t=4), func=ACT.Tanh, scale=sign
+                    out=bounded[:], in_=tiles[jb][:].rearrange("j (p t) -> j t p", t=4), func=ACT.Tanh, scale=sign
                 )
                 made.append(bounded)
             return made
@@ -238,12 +235,10 @@ def tile_list_levelling_traverse_features_kernel(
         fore_at = [[base + 8 * KB + 2 * KB * jb for jb in range(JB)] for base in (REG_B, REG_C)]
         back_at = [SPARE + 4 * KB, SPARE + 6 * KB, REG_B + 6 * KB, REG_D + 14 * KB]
 
-        late_back_at = [REG_A + 8 * KB + 2 * KB * jb for jb in range(JB)]
-
         def pick_d(first, last):
             d_picked.extend(pick("d_picked%d" % i, picked_at[i], d_win[i], pos3_sb) for i in range(first, last))
 
-        d_at = [REG_D, V2_0, V2_1, REG_F, REG_G, ring(1), ring(2), ring(3)]
+        d_at = [REG_D, V2_0, V2_1, REG_F, ring(0), ring(1), ring(2), ring(3)]
         d_win = [d_window(i, d_at[i]) for i in range(TILES)]
         d_picked = []
         pick_d(0, 2)
@@ -253,15 +248,13 @@ def tile_list_levelling_traverse_features_kernel(
         v2.append(gather_words("v2_1", V2_1, tab2_sb[1], offs2_sb, 1))
         pick_d(3, 5)
         wo_raw0 = load_weight("wo_raw0", REG_F, wo[0:K, :])
-        gain_row = placed("gain_row", [P, K], F32, REG_G)
-        nc.sync.dma_start(out=gain_row[:], in_=gain[0:K].partition_broadcast(P))
         wa_bf = round_weight("wa_bf", WA_BF, wa_raw)
         wo_raw1 = load_weight("wo_raw1", REG_A, wo[K : 2 * K, :])
 
         b_win = [b_window(0, ring(4), X), b_window(1, ring(5), X + 2), b_window(2, ring(6), Y), b_window(3, WA_CODES, Y + 2)]
         neg_b = [pick("neg_b%d" % i, neg_b_at[i], b_win[i], pos2_sb) for i in range(GROUP)]
         b_win.extend([b_window(4, ring(7), X), b_window(5, ring(0), X + 2)])
-        fore = [differences("fore0_", Y, d_picked, neg_b, -1.0, fore_at[0], AS_IS)]
+        fore = [differences("fore0_", Y, d_picked, neg_b, -1.0, fore_at[0])]
         b_win.extend([b_window(6, ring(4), X), b_window(7, ring(5), X + 2)])
 
         wa_codes, wa_sc = quantise_weight("wa", WA_CODES, wa_bf)
@@ -272,56 +265,43 @@ def tile_list_levelling_traverse_features_kernel(
 
         a_at = [ring(k) for k in (6, 1, 2, 3, 7, 0, 4, 5)]
         a_win = [a_window(i, a_at[i]) for i in range(TILES)]
-        fore.append(differences("fore1_", Y, d_picked[GROUP:], neg_b[GROUP:], -1.0, fore_at[1], BY_BYTE))
+        fore.append(differences("fore1_", Y, d_picked[GROUP:], neg_b[GROUP:], -1.0, fore_at[1]))
         a_picked = [pick("a_picked%d" % i, picked_at[i], a_win[i], pos1_sb) for i in range(TILES)]
-        wo_q = [quantise_weight("wo%d" % g, a_at[(3, 7)[g]], wo_bf[g]) for g in range(2)]
+        wo_q = [quantise_weight("wo%d" % g, a_at[TILES - 2 + g], wo_bf[g]) for g in range(2)]
 
         z_codes = kept("z_codes", [P, 2, J], U32)
         z_sc = kept("z_sc", [P, 2, J], U8)
 
-        def quantise_z(g, z_bf):
+        def open_sums(g, banks):
+            tiles = [bank_tile("sum%d_%d" % (g, jb), banks + jb) for jb in range(JB)]
+            for jb in range(JB):
+                for t in range(4):
+                    turn(tiles[jb], t, fore[g][jb][:, t, :], t == 0, False)
+            return tiles
+
+        def finish_z(g, tiles, back):
+            z_bf = placed("z_bf%d" % g, [P, J, 4], BF16, Z_BF + 4 * KB * g)
+            for jb in range(JB):
+                for t in range(4):
+                    turn(tiles[jb], t, back[jb][:, t, :], False, t == 3)
+                nc.vector.tensor_tensor(
+                    out=z_bf[:, rows(jb), :],
+                    in0=tiles[jb][:].rearrange("p (t j) -> p j t", t=4),
+                    in1=gain_sb[:, g, :].unsqueeze(1).to_broadcast([P, P, 4]),
+                    op=ALU.mult,
+                )
             nc.vector.quantize_mx(
                 out=z_codes[:, g, :].bitcast(FP8X4), scales=z_sc[:, g, :], in_=z_bf[:].rearrange("p j t -> p (j t)")
             )
 
-        z_bf = [placed("z_bf%d" % g, [P, J, 4], BF16, Z_BF + 4 * KB * g) for g in range(2)]
-        back0 = differences("back0_", X, neg_b, a_picked, 1.0, back_at, AS_IS)
-        totals = []
-        for jb in range(JB):
-            total = placed("total%d" % jb, [P, BANK], F32, REG_A + 2 * KB * jb)
-            nc.gpsimd.tensor_tensor(
-                out=total[:], in0=fore[0][jb][:].rearrange("j t p -> j (t p)"),
-                in1=back0[jb][:].rearrange("j t p -> j (t p)"), op=ALU.add,
-            )
-            totals.append(total)
-        sums = [bank_tile("sum%d" % jb, Y + jb) for jb in range(JB)]
-        for jb in range(JB):
-            for t in range(4):
-                turn(sums[jb], t, fore[1][jb][:, t, :], t == 0, False)
-        back1 = differences("back1_", X, neg_b[GROUP:], a_picked[GROUP:], 1.0, late_back_at, BY_BYTE)
-        for jb in range(JB):
-            z_t = placed("z_t%d" % jb, [P, BANK], BF16, REG_G + 2 * KB + KB * jb)
-            nc.vector.tensor_tensor(out=z_t[:], in0=totals[jb][:], in1=gain_row[:], op=ALU.mult)
-            bank = bank_tile("z_bank%d" % jb, X + jb)
-            for u in range(2):
-                nc.tensor.transpose(bank[:, rows(u)], z_t[:].bitcast(F32)[:, u : 2 * P : 2], identity[:])
-            nc.scalar.copy(
-                out=z_bf[0][:, rows(jb), :].bitcast(F32), in_=bank[:, 0 : 2 * P].rearrange("p (u j) -> p j u", u=2)
-            )
-        for jb in range(JB):
-            for t in range(4):
-                turn(sums[jb], t, back1[jb][:, t, :], False, t == 3)
-            nc.vector.tensor_tensor(
-                out=z_bf[1][:, rows(jb), :],
-                in0=sums[jb][:].rearrange("p (t j) -> p j t", t=4),
-                in1=gain_sb[:].unsqueeze(1).to_broadcast([P, P, 4]),
-                op=ALU.mult,
-            )
-        quantise_z(0, z_bf[0])
-        quantise_z(1, z_bf[1])
+        sums = open_sums(0, X)
+        back = differences("back0_", Y, neg_b, a_picked, 1.0, back_at)
+        finish_z(0, sums, back)
+        back = differences("back1_", Y, neg_b[GROUP:], a_picked[GROUP:], 1.0, back_at)
+        finish_z(1, open_sums(1, X), back)
 
         for i in range(TILES):
-            bank = bank_tile("y%d" % i, X + i)
+            bank = bank_tile("y%d" % i, (Y + i) % BANKS)
             for g in range(2):
                 codes, scales = wo_q[g]
                 nc.tensor.matmul_mx(

from contextlib import ExitStack

import concourse.mybir as mybir
from concourse.masks import make_identity

K, K2, H, T, S, J = 512, 1024, 1024, 4096, 1024, 512
FLOPS = 2 * (K * H * S + K2 * H * S + K * H * S + H * H * J)

F32 = mybir.dt.float32
BF16 = mybir.dt.bfloat16
I32 = mybir.dt.int32
U32 = mybir.dt.uint32
U16 = mybir.dt.uint16
U8 = mybir.dt.uint8
FP8X4 = mybir.dt.float8_e4m3fn_x4
FP4X4 = mybir.dt.float4_e2m1fn_x4
ALU = mybir.AluOpType
ACT = mybir.ActivationFunctionType

P = 128
BANK = 512
TILES = H // P
GROUP = 4
JB = J // P
BANKS = 8


KB = 1024
REG_A, REG_B, REG_C, REG_D, REG_E = 0, 16 * KB, 32 * KB, 48 * KB, 64 * KB
RING = 80 * KB
V2_0, V2_1, WA_CODES, V = 112 * KB, 116 * KB, 120 * KB, 124 * KB
WA_BF, WO_BF, Z_BF = 128 * KB, 136 * KB, 152 * KB
SPARE = 160 * KB
V3 = 168 * KB
REG_F = 172 * KB
WB = 188 * KB
X, Y = 0, 4


def tile_list_levelling_traverse_features_kernel(
    tc, tab_words, tab_scales, tab2_words, tab2_scales, tab3_words, tab3_scales, offs, offs2, offs3,
    pos1, pos2, pos3, wa, wb_words, wb_scales, wd_words, wd_scales, gain, wo, out,
):
    nc = tc.nc
    with ExitStack() as ctx:
        keep = ctx.enter_context(tc.tile_pool(name="keep", bufs=1))
        arena = ctx.enter_context(tc.tile_pool(name="arena", bufs=1))
        psum = ctx.enter_context(tc.psum_pool(name="psum", bufs=1))

        def placed(name, shape, dtype, offset):
            return arena.tile(shape, dtype, name=name, offset=offset, align_bytes=64)

        def kept(name, shape, dtype):
            return keep.tile(shape, dtype, name=name, align_bytes=64)

        def bank_tile(name, k):
            return psum.tile([P, BANK], F32, name=name, tag="bank%d" % k)

        def rows(i):
            return slice(i * P, (i + 1) * P)

        def load_list(name, src):
            tile = keep.tile(list(src.shape), U16, name=name)
            nc.sync.dma_start(tile[:], src)
            return tile

        def load_words(name, offset, src):
            tile = placed(name, [P, T], I32, offset)
            nc.sync.dma_start(out=tile[:], in_=src.rearrange("p t i -> p (t i)").bitcast(I32))
            return tile

        def load_plane(queue, tile, first, src):
            for q in range(4):
                row = 32 * q + first
                queue.dma_start(out=tile[row : row + 4, :].bitcast(I32), in_=src[4 * q : 4 * q + 4, :].bitcast(I32))

        def gather_words(name, offset, table, offsets, pieces):
            tile = placed(name, [P, S], U32, offset)
            n = S // pieces
            for c in range(pieces):
                nc.vector.tensor_copy(
                    tile[:, c * n : (c + 1) * n],
                    table[:].bitcast(U32).indirect(offsets[:, c * n // 16 : (c + 1) * n // 16]),
                )
            return tile

        def load_half(raw, src, h):
            nc.sync.dma_start(
                out=raw[:, h], in_=src[:, h * BANK : (h + 1) * BANK].rearrange("(p i) n -> p i n", i=4)
            )

        def load_weight(name, offset, src):
            raw = placed(name, [P, 2, 4, BANK], F32, offset)
            for h in range(2):
                load_half(raw, src, h)
            return raw

        def round_weight(name, offset, raw):
            halves = []
            for h in range(2):
                rounded = placed("%s%d" % (name, h), [P, BANK, 4], BF16, offset + 4 * KB * h)
                nc.gpsimd.tensor_scalar(
                    out=rounded[:], in0=raw[:, h].rearrange("p i n -> p n i"),
                    scalar1=1.0, scalar2=0.0, op0=ALU.mult, op1=ALU.add,
                )
                halves.append(rounded)
            return halves

        def quantise_weight(name, offset, halves):
            codes = placed(name + "_codes", [P, H], U32, offset)
            scales = kept(name + "_scales", [P, H], U8)
            for h in range(2):
                nc.vector.quantize_mx(
                    out=codes[:, h * BANK : (h + 1) * BANK].bitcast(FP8X4),
                    scales=scales[:, h * BANK : (h + 1) * BANK],
                    in_=halves[h][:].rearrange("p n i -> p (n i)"),
                )
            return codes, scales

        offs3_sb = load_list("offs3_sb", offs3)
        offs2_sb = load_list("offs2_sb", offs2)
        offs_sb = load_list("offs_sb", offs)
        pos3_sb = load_list("pos3_sb", pos3)
        pos2_sb = load_list("pos2_sb", pos2)
        pos1_sb = load_list("pos1_sb", pos1)
        gain_sb = kept("gain_sb", [P, 2, 4], F32)
        nc.sync.dma_start(out=gain_sb[:], in_=gain.rearrange("(b p t) -> p b t", p=P, t=4))
        wd_sb = [kept("wd_sb%d" % h, [P, BANK], U32) for h in range(2)]
        for h in range(2):
            nc.sync.dma_start(
                out=wd_sb[h][:].bitcast(I32),
                in_=wd_words[0, :, h * BANK : (h + 1) * BANK, :].rearrange("p c i -> p (c i)").bitcast(I32),
            )

        tab3_sc = placed("tab3_sc", [P, T], U8, REG_B)
        tab2_sc = placed("tab2_sc", [P, T], U8, WB)
        tab_sc = placed("tab_sc", [P, T], U8, REG_C)
        wd_sc = kept("wd_sc", [P, H], U8)
        wb_sc = kept("wb_sc", [P, 2, H], U8)
        v2_sc1 = kept("v2_sc1", [P, S], U8)
        for plane in (wd_sc, tab3_sc, tab2_sc, tab_sc, v2_sc1):
            nc.vector.memset(plane[:].bitcast(I32), 0)
        nc.vector.memset(wb_sc[:].rearrange("p a c -> p (a c)").bitcast(I32), 0)
        load_plane(nc.sync, tab3_sc, 12, tab3_scales[0])
        for q in range(4):
            nc.sync.dma_start(
                out=tab2_sc[32 * q : 32 * q + 8, :].bitcast(I32), in_=tab2_scales[:, 4 * q : 4 * q + 4, :].bitcast(I32)
            )
        load_plane(nc.sync, tab_sc, 8, tab_scales[0])
        tab3_sb = load_words("tab3_sb", REG_A, tab3_words[0])
        load_plane(nc.gpsimd, wd_sc, 0, wd_scales[0])
        for q in range(4):
            nc.sync.dma_start(
                out=wb_sc[32 * q : 32 * q + 4].bitcast(I32),
                in_=wb_scales[:, 4 * q : 4 * q + 4, :].rearrange("a r c -> r a c").bitcast(I32),
            )

        def gather_scales(name, plane, offsets):
            tile = kept(name, [P, S], U8)
            nc.vector.tensor_copy(tile[:], plane[:].indirect(offsets[:]))
            return tile

        v3_sc = gather_scales("v3_sc", tab3_sc, offs3_sb)
        v2_sc = [gather_scales("v2_sc0", tab2_sc, offs2_sb), v2_sc1]
        for r in range(4):
            nc.gpsimd.dma_start(out=v2_sc1[r:P:32, :].bitcast(I32), in_=v2_sc[0][4 + r : P : 32, :].bitcast(I32))
        identity = kept("identity", [P, P], F32)
        make_identity(nc, identity[:])
        v_sc = gather_scales("v_sc", tab_sc, offs_sb)
        tab2_sb = [load_words("tab2_sb%d" % a, (REG_B, REG_C)[a], tab2_words[a]) for a in range(2)]
        wb_sb = placed("wb_sb", [P, 2, 2 * H], U8, WB)
        nc.sync.dma_start(out=wb_sb[:].bitcast(I32), in_=wb_words.rearrange("a p c -> p a c").bitcast(I32))
        v3 = gather_words("v3", V3, tab3_sb, offs3_sb, 2)
        wa_raw = load_weight("wa_raw", REG_A, wa)

        def produce(name, offset, first_bank, passes, sign):
            window = placed(name, [P, S], F32, offset)
            for h in range(2):
                cols = slice(h * BANK, (h + 1) * BANK)
                bank = bank_tile("%s_bank%d" % (name, h), first_bank + h)
                for a, (w, w_sc, x, x_sc) in enumerate(passes):
                    nc.tensor.matmul_mx(
                        out=bank[:], lhsT=w, lhsT_scale=w_sc, rhs=x[:, cols].bitcast(FP8X4), rhs_scale=x_sc[:, cols],
                        start=(a == 0), stop=(a == len(passes) - 1),
                    )
                nc.scalar.activation(out=window[:, cols], in_=bank[:], func=ACT.Copy, scale=sign)
            return window

        def pick(name, offset, window, positions):
            picked = placed(name, [P, J], F32, offset)
            nc.vector.tensor_copy(picked[:], window[:].indirect(positions[:]))
            return picked

        def turn(bank, region, src, start, stop):
            nc.tensor.matmul(bank[:, rows(region)], lhsT=src, rhs=identity[:], is_transpose=True, start=start, stop=stop)

        def differences(name, banks, first, second, sign, offsets):
            made = []
            tiles = [bank_tile("%s_bank%d" % (name, jb), banks + jb) for jb in range(JB)]
            for jb in range(JB):
                for i in range(GROUP):
                    turn(tiles[jb], i, first[i][:, rows(jb)], i == 0, False)
            for i in range(GROUP):
                for jb in range(JB):
                    turn(tiles[jb], i, second[i][:, rows(jb)], False, i == GROUP - 1)
            for jb in range(JB):
                bounded = placed("%s%d" % (name, jb), [P, 4, P], F32, offsets[jb])
                nc.scalar.activation(
                    out=bounded[:], in_=tiles[jb][:].rearrange("j (p t) -> j t p", t=4), func=ACT.Tanh, scale=sign
                )
                made.append(bounded)
            return made

        def ring(k):
            return RING + 4 * KB * k

        def d_window(i, offset):
            passes = [(wd_sb[i // GROUP][:, rows(i % GROUP)].bitcast(FP8X4), wd_sc[:, rows(i)], v3, v3_sc[12:P])]
            return produce("d%d" % i, offset, 2 * i % BANKS, passes, 1.0)

        def b_window(i, offset, first_bank):
            passes = [
                (wb_sb[:, a, 2 * i * P : 2 * (i + 1) * P].bitcast(FP4X4), wb_sc[:, a, rows(i)], v2[a], v2_sc[a][:])
                for a in range(2)
            ]
            return produce("b%d" % i, offset, first_bank, passes, -1.0)

        def a_window(i, offset):
            passes = [(wa_codes[:, rows(i)].bitcast(FP8X4), wa_sc[:, rows(i)], v, v_sc[8:P])]
            return produce("a%d" % i, offset, (Y + 2 * i) % BANKS, passes, 1.0)

        picked_at = [SPARE, SPARE + 2 * KB, REG_B, REG_C, REG_C + 2 * KB, REG_D, REG_D + 2 * KB, REG_D + 4 * KB]
        neg_b_at = [REG_B + 2 * KB, REG_B + 4 * KB, REG_C + 4 * KB, REG_C + 6 * KB]
        neg_b_at = neg_b_at + [REG_D + 6 * KB + 2 * KB * i for i in range(GROUP)]
        fore_at = [[base + 8 * KB + 2 * KB * jb for jb in range(JB)] for base in (REG_B, REG_C)]
        back_at = [SPARE + 4 * KB, SPARE + 6 * KB, REG_B + 6 * KB, REG_D + 14 * KB]

        def pick_d(first, last):
            d_picked.extend(pick("d_picked%d" % i, picked_at[i], d_win[i], pos3_sb) for i in range(first, last))

        d_at = [REG_D, V2_0, V2_1, REG_F, ring(0), ring(1), ring(2), ring(3)]
        d_win = [d_window(i, d_at[i]) for i in range(TILES)]
        d_picked = []
        pick_d(0, 2)
        tab_sb = load_words("tab_sb", REG_D, tab_words[0])
        v2 = [gather_words("v2_0", V2_0, tab2_sb[0], offs2_sb, 1)]
        pick_d(2, 3)
        v2.append(gather_words("v2_1", V2_1, tab2_sb[1], offs2_sb, 1))
        pick_d(3, 5)
        wo_raw0 = load_weight("wo_raw0", REG_F, wo[0:K, :])
        wa_bf = round_weight("wa_bf", WA_BF, wa_raw)
        wo_raw1 = load_weight("wo_raw1", REG_A, wo[K : 2 * K, :])

        b_win = [b_window(0, ring(4), X), b_window(1, ring(5), X + 2), b_window(2, ring(6), Y), b_window(3, WA_CODES, Y + 2)]
        neg_b = [pick("neg_b%d" % i, neg_b_at[i], b_win[i], pos2_sb) for i in range(GROUP)]
        b_win.extend([b_window(4, ring(7), X), b_window(5, ring(0), X + 2)])
        fore = [differences("fore0_", Y, d_picked, neg_b, -1.0, fore_at[0])]
        b_win.extend([b_window(6, ring(4), X), b_window(7, ring(5), X + 2)])

        wa_codes, wa_sc = quantise_weight("wa", WA_CODES, wa_bf)
        v = gather_words("v", WA_BF, tab_sb, offs_sb, 1)
        wo_bf = [round_weight("wo_bf0_", WA_BF + 4 * KB, wo_raw0), round_weight("wo_bf1_", WA_BF + 12 * KB, wo_raw1)]
        pick_d(5, 8)
        neg_b.extend(pick("neg_b%d" % i, neg_b_at[i], b_win[i], pos2_sb) for i in range(GROUP, TILES))

        a_at = [ring(k) for k in (6, 1, 2, 3, 7, 0, 4, 5)]
        a_win = [a_window(i, a_at[i]) for i in range(TILES)]
        fore.append(differences("fore1_", Y, d_picked[GROUP:], neg_b[GROUP:], -1.0, fore_at[1]))
        a_picked = [pick("a_picked%d" % i, picked_at[i], a_win[i], pos1_sb) for i in range(TILES)]
        wo_q = [quantise_weight("wo%d" % g, a_at[TILES - 2 + g], wo_bf[g]) for g in range(2)]

        z_codes = kept("z_codes", [P, 2, J], U32)
        z_sc = kept("z_sc", [P, 2, J], U8)

        def open_sums(g, banks):
            tiles = [bank_tile("sum%d_%d" % (g, jb), banks + jb) for jb in range(JB)]
            for jb in range(JB):
                for t in range(4):
                    turn(tiles[jb], t, fore[g][jb][:, t, :], t == 0, False)
            return tiles

        def finish_z(g, tiles, back):
            z_bf = placed("z_bf%d" % g, [P, J, 4], BF16, Z_BF + 4 * KB * g)
            for jb in range(JB):
                for t in range(4):
                    turn(tiles[jb], t, back[jb][:, t, :], False, t == 3)
                nc.vector.tensor_tensor(
                    out=z_bf[:, rows(jb), :],
                    in0=tiles[jb][:].rearrange("p (t j) -> p j t", t=4),
                    in1=gain_sb[:, g, :].unsqueeze(1).to_broadcast([P, P, 4]),
                    op=ALU.mult,
                )
            nc.vector.quantize_mx(
                out=z_codes[:, g, :].bitcast(FP8X4), scales=z_sc[:, g, :], in_=z_bf[:].rearrange("p j t -> p (j t)")
            )

        sums = open_sums(0, X)
        back = differences("back0_", Y, neg_b, a_picked, 1.0, back_at)
        finish_z(0, sums, back)
        back = differences("back1_", Y, neg_b[GROUP:], a_picked[GROUP:], 1.0, back_at)
        finish_z(1, open_sums(1, X), back)

        for i in range(TILES):
            bank = bank_tile("y%d" % i, (Y + i) % BANKS)
            for g in range(2):
                codes, scales = wo_q[g]
                nc.tensor.matmul_mx(
                    out=bank[:], lhsT=codes[:, rows(i)].bitcast(FP8X4), lhsT_scale=scales[:, rows(i)],
                    rhs=z_codes[:, g, :].bitcast(FP8X4), rhs_scale=z_sc[:, g, :], start=(g == 0), stop=(g == 1),
                )
            result = placed("result%d" % i, [P, J], F32, REG_E + 2 * KB * i)
            nc.vector.tensor_tensor(out=result[:], in0=bank[:], in1=neg_b[i][:], op=ALU.subtract)
            nc.sync.dma_start(out=out[rows(i), :], in_=result[:])
